import numpy as np, ml_dtypes
CORES = [23,119,17,113]
N = 4
import mx_ref
BF = ml_dtypes.bfloat16
def entries(a):
    return np.ascontiguousarray(a.T).reshape(-1)
def table(e):
    return np.ascontiguousarray(np.reshape(e, (-1, 16)).T).astype(np.int32)
def tile(rs):
    return np.stack(rs, axis=2).reshape(128, -1).astype(BF)
def cut(t, i, w=512):
    return t[:, w * i:w * i + w]
def f(rng, *shape):
    return mx_ref.flush((rng.standard_normal(shape, dtype=np.float32) * np.exp2(rng.integers(-2, 3, shape[:-1] + (1,)))).astype(BF))
def wide(rng, *shape, cols=0):
    v = rng.standard_normal(shape, dtype=np.float32) * np.exp2(rng.integers(-12, 13, shape)).astype(np.float32)
    if cols: v *= np.repeat(np.exp2(rng.integers(-cols, cols + 1, shape[:-2] + (1, shape[-1] // 4))) * (rng.random(shape[:-2] + (1, shape[-1] // 4)) > 0.0625), 4, axis=-1).astype(np.float32)
    return mx_ref.flush(v.astype(BF))
T, TG, C1, C2 = 512, 256, 320, 64
def layer(rng, C, M, own=0.25, full=False, hub=False, neg=None):
    snd = np.full((N, N, C), -1); src = np.zeros((N, M, 4), int)
    for s in range(N):
        for r in range(N):
            if s != r and own < 1:
                n = C if full else rng.integers(1, C + 1)
                snd[s, r, rng.permutation(C)[:n]] = rng.choice(T, n, replace=False)
    h, k, c = rng.integers(0, N), rng.integers(0, T), rng.integers(0, C, N)
    if hub:
        for r in range(N):
            if r != h: snd[h, r, c[r]] = k
    for r in range(N):
        src[r] = rng.integers(0, T, (M, 4))
        if own < 1:
            far = T + np.flatnonzero(snd[:, r].reshape(-1) >= 0)
            src[r] = np.where(rng.random((M, 4)) < own, src[r], rng.choice(far, (M, 4)))
        if hub:
            e = k if r == h else T + h * C + c[r]
            src[r][:, 0] = e; src[r][rng.permutation(M)[:M // 4]] = e
            src[r] = rng.permuted(src[r], axis=1)
        if neg is not None:
            bad = np.flatnonzero(np.concatenate([neg[r]] + [(snd[s, r] >= 0) & neg[s][snd[s, r]] for s in range(N)]))
            src[r][rng.permutation(M)[:M // 2]] = rng.choice(bad, (M // 2, 4))
    return np.stack([table(a) for a in snd]), np.stack([table(a) for a in src])
def lists(rng, neg=None, **o):
    a, b = layer(rng, C1, T, neg=neg, **o); c, e = layer(rng, C2, TG, **o)
    return {"snd1": a, "src1": b, "snd2": c, "src2": e}
def setup_inputs(rng):
    return {"x": f(rng, N, 128, 4 * T), "w1": np.repeat(f(rng, 1, 128, 4 * 512), N, axis=0), "w2": np.repeat(f(rng, 1, 128, 512), N, axis=0), **lists(rng)}
def setup_inputs_foreign(rng):
    return {**setup_inputs(rng), **lists(rng, own=0, full=True)}
def setup_inputs_hub(rng):
    return {**setup_inputs(rng), **lists(rng, hub=True)}
def setup_inputs_negative(rng):
    d = setup_inputs(rng)
    neg = np.stack([rng.permutation(T) < T // 2 for r in range(N)])
    v = np.abs(d["x"]).reshape(N, 128, T, 4)
    d["x"] = np.where(neg[:, None, :, None], -v, v).reshape(N, 128, 4 * T)
    d["w1"] = np.abs(d["w1"])
    return {**d, **lists(rng, neg=neg)}
def setup_inputs_self(rng):
    return {**setup_inputs(rng), **lists(rng, own=1)}
def setup_inputs_spread(rng):
    d = setup_inputs(rng); d["x"] = wide(rng, N, 128, 4 * T); return d
def check_inputs(d):
    b = []
    for k in ("w1", "w2"):
        if any(d[k][r].tobytes() != d[k][0].tobytes() for r in range(N)): b.append(k)
    for l, C in (("1", C1), ("2", C2)):
        snd = np.stack([entries(a) for a in d["snd" + l]]).reshape(N, N, C)
        if snd.min() < -1 or snd.max() >= T: b.append("snd" + l)
        for r in range(N):
            if (snd[r, r] != -1).any(): b.append("snd" + l)
            ok = np.concatenate([np.ones(T, bool), snd[:, r].reshape(-1) >= 0])
            e = entries(d["src" + l][r])
            if e.min() < 0 or e.max() >= T + N * C or not ok[e].all(): b.append("src" + l)
    return b
def most(v, snd, src, r, C):
    a = np.concatenate([v[r]] + [v[s][:, entries(snd[s])[r * C:r * C + C]] for s in range(N)], axis=1)
    return a[:, entries(src[r])].reshape(128, -1, 4).max(axis=2)
def reference(x, w1, w2, snd1, src1, snd2, src2):
    q = [mx_ref.quantize(x[r]) for r in range(N)]
    Z = [[mx_ref.matmul(mx_ref.quantize(cut(w1[r], i)), q[r]) for r in range(N)] for i in range(4)]
    U = []
    for r in range(N):
        h = tile([np.maximum(most(Z[i], snd1, src1, r, C1), np.float32(0)) * np.float32(0.05) for i in range(4)])
        U.append(mx_ref.matmul(mx_ref.quantize(w2[r]), mx_ref.quantize(h)))
    return {"y": np.stack([most(U, snd2, src2, r, C2) for r in range(N)])}

@@ -1,0 +1,348 @@
+import numpy as np
+from concourse.bass import DstId, RemoteDMATransfer, IndirectOffsetOnAxis
+from concourse.mybir import dt, AluOpType, ActivationFunctionType
+
+N, NODES, TG, C1, C2 = 4, 512, 256, 320, 64
+W1T = NODES + N * C1
+W2T = NODES + N * C2
+F8 = "float8_e4m3fn_x4"
+SCRATCH = {
+    "xb": ("sbuf", [128, 2048], "bfloat16"), "xq": ("sbuf", [128, 512], F8), "xp": ("sbuf", [128, 512], "uint8"),
+    "w1b": ("sbuf", [128, 2048], "bfloat16"), "w1q": ("sbuf", [128, 512], F8), "w1p": ("sbuf", [128, 512], "uint8"),
+    "w2b": ("sbuf", [128, 512], "bfloat16"), "w2q": ("sbuf", [128, 128], F8), "w2p": ("sbuf", [128, 128], "uint8"),
+    "xs": ("sbuf", [128, 12 * C1], "bfloat16"), "xsq": ("sbuf", [128, 3 * C1], F8), "xsp": ("sbuf", [128, 3 * C1], "uint8"),
+    "c1": ("sbuf", [128, 3 * C1], F8), "p1": ("sbuf", [128, 3 * C1], "uint8"),
+    "r0": ("sbuf", [128, W1T], "bfloat16"), "r1": ("sbuf", [128, W1T], "bfloat16"),
+    "r2": ("sbuf", [128, W1T], "bfloat16"), "r3": ("sbuf", [128, W1T], "bfloat16"),
+    "h": ("sbuf", [128, 2048], "bfloat16"), "hq": ("sbuf", [128, 512], F8), "hp": ("sbuf", [128, 512], "uint8"),
+    "hs": ("sbuf", [128, 12 * C2], "bfloat16"), "hsq": ("sbuf", [128, 3 * C2], F8), "hsp": ("sbuf", [128, 3 * C2], "uint8"),
+    "c2": ("sbuf", [128, 3 * C2], F8), "p2": ("sbuf", [128, 3 * C2], "uint8"),
+    "mask": ("sbuf", [128, 1536], "bfloat16"),
+    "bs": ("sbuf", [128, 4 * 576], "bfloat16"), "bt": ("sbuf", [128, 4 * 576], "bfloat16"),
+    "bh": ("sbuf", [128, 2 * 1536], "bfloat16"), "bi": ("sbuf", [128, 2 * 1536], "bfloat16"),
+    "u": ("sbuf", [128, W2T], "float32"), "yb": ("sbuf", [128, TG], "float32"),
+    "sl": ("sbuf", [128, 80], "int32"), "sl4": ("sbuf", [128, 80], "int32"), "so": ("sbuf", [128, 320], "uint16"),
+    "l1": ("sbuf", [16, 128], "int32"), "lc1": ("sbuf", [16, 128], "int32"), "d1": ("dram", [16, 128], "int32"),
+    "e1": ("sbuf", [128, 128], "int32"), "o1": ("sbuf", [128, 128], "uint16"),
+    "l2": ("sbuf", [16, 64], "int32"), "lc2": ("sbuf", [16, 64], "int32"), "d2": ("dram", [16, 64], "int32"),
+    "e2": ("sbuf", [128, 64], "int32"), "o2": ("sbuf", [128, 64], "uint16"),
+    "li": ("sbuf", [32, 64], "int32"), "lf": ("sbuf", [32, 64], "float32"), "lt": ("sbuf", [32, 64], "float32"),
+    "t4": ("dram", [512, 4], "float32"),
+    "dsn": ("dram", [16, 12], "int32"), "ix": ("sbuf", [128, 2], "int32"), "ixc": ("sbuf", [128, 2], "int32"),
+    "cr": ("sbuf", [128, 8], "float32"), "ec": ("sbuf", [128, 48], "float32"), "oc": ("sbuf", [128, 48], "uint16"),
+    "ps": ("psum", [128, 4096], "float32"),
+}
+SEMAPHORES = ["cv", "cs", "ct", "d_snd", "d_x", "g_l", "d_dsn", "d_ix", "d_l2", "d_w1", "d_w2", "d_t4", "d_d1", "d_e1",
+              "d_d2", "d_e2", "g_i", "d_ec", "d_y", "a1_0", "a1_1", "a1_2", "a2", "sent"]
+
+
+def rank_program(g, core, T, topo):
+    r = T.rank_of(core)
+    if r is None:
+        return
+    V, S, P, Y = g.vector, g.scalar, g.tensor, g.sync
+    queues = {"g": g, "V": V, "S": S, "P": P, "Y": Y}
+    MAX, MULT, ADD = AluOpType.max, AluOpType.mult, AluOpType.add
+    COPY, RELU = ActivationFunctionType.Copy, ActivationFunctionType.Relu
+    U8 = dt.uint8
+    count = {}
+    seen = {}
+
+    def done(sem, ins, k=1):
+        ins.then_inc(T.sem[sem], k)
+        count[sem] = count.get(sem, 0) + k
+        return (sem, count[sem])
+
+    def need(q, *toks):
+        for sem, k in toks:
+            if seen.get((q, sem), 0) < k:
+                queues[q].wait_ge(T.sem[sem], k)
+                seen[(q, sem)] = k
+
+    def v(ins): return done("cv", ins)
+    def s(ins): return done("cs", ins)
+    def p(ins): return done("ct", ins)
+    def dma(sem, ins): return done(sem, ins, 16)
+
+    others = [d for d in range(N) if d != r]
+    me = T.cores[r]
+    far = [d for d in others if topo.chip(T.cores[d]) != topo.chip(me)]
+    far.sort(key=lambda d: topo.die(T.cores[d]) != topo.die(me))
+    near = [d for d in others if d not in far]
+    order = [far[0], far[1], near[0]]
+    arrive = [far[0], near[0], far[1]]
+    far_eng = topo.engines(me, T.cores[far[0]])
+    near_eng = [e for e in topo.engines(me, T.cores[near[0]]) if e not in far_eng]
+    half = len(far_eng) // 2
+
+    def bits(es): return sum(1 << e for e in es)
+    def slot(a, b): return a - (1 if a > b else 0)
+    runs = []
+    for d in others:
+        if runs and runs[-1][0] + runs[-1][1] == d: runs[-1][1] += 1
+        else: runs.append([d, 1])
+
+    for k in range(4):
+        dma("d_snd", Y.dma_start(out=T.sl[16 * k:16 * k + 16, :], in_=T.snd1[:, :]))
+        t_snd = dma("d_snd", S.dma_start(out=T.sl[16 * (k + 4):16 * (k + 4) + 16, :], in_=T.snd1[:, :]))
+    dma("d_x", Y.dma_start(out=T.xb[:, 0:1024], in_=T.x[:, 0:1024]))
+    t_x = dma("d_x", S.dma_start(out=T.xb[:, 1024:2048], in_=T.x[:, 1024:2048]))
+    for k in range(2):
+        dma("g_l", g.dma_start(out=T.li[16 * k:16 * k + 16, :], in_=T.src1[:, 64 * k:64 * k + 64]))
+    t_l = dma("g_l", g.dma_start(out=T.l1[:, :], in_=T.src1[:, :]))
+    c = 0
+    for d, n in runs:
+        t_dsn = dma("d_dsn", Y.dma_start(out=T.dsn[:, c:c + 4 * n], in_=T.snd2[:, 4 * d:4 * d + 4 * n]))
+        c += 4 * n
+    dma("d_w1", Y.dma_start(out=T.w1b[:, 0:1024], in_=T.w1[:, 0:1024]))
+    t_w1 = dma("d_w1", S.dma_start(out=T.w1b[:, 1024:2048], in_=T.w1[:, 1024:2048]))
+    t_l2 = dma("d_l2", Y.dma_start(out=T.l2[:, :], in_=T.src2[:, :]))
+    t_w2 = dma("d_w2", Y.dma_start(out=T.w2b[:, :], in_=T.w2[:, :]))
+    need("Y", t_dsn)
+    t_ix = dma("d_ix", Y.dma_start(out=T.ix[0:96, :], in_=T.dsn[:, :]))
+
+    R = [T["r%d" % i] for i in range(4)]
+    t_one = v(V.memset(T.mask[:, :], 1.0))
+    for i in range(4):
+        t_r = v(V.memset(R[i][:, NODES + C1 * r:NODES + C1 * r + C1], 0.0))
+    t_u = v(V.memset(T.u[:, NODES + C2 * r:NODES + C2 * r + C2], 0.0))
+    need("V", t_one)
+    t_mask = v(V.memset(T.mask[:, 0::3], 0.0))
+
+    need("V", t_snd)
+    t_a = v(V.tensor_scalar(out=T.sl4[:, :], in0=T.sl[:, :], scalar1=0.0, scalar2=4.0, op0=MAX, op1=MULT))
+    need("V", t_a)
+    for t in range(4):
+        t_so = v(V.tensor_scalar(out=T.so[:, 80 * t:80 * t + 80], in0=T.sl4[:, :], scalar1=float(t), scalar2=None, op0=ADD))
+
+    def listed(j, t):
+        d = order[j]
+        return (T.xs[:, 4 * C1 * j + t:4 * C1 * (j + 1):4], T.xb[:, 0:2048].indirect(T.so[:, 80 * t + 20 * d:80 * t + 20 * d + 20]))
+
+    def to(d):
+        rid, pid, _ = topo.addr(T.cores[d])
+        return rid, pid
+
+    def send1(kind, j):
+        d = order[j]
+        k = slot(r, d)
+        rid, pid = to(d)
+        a, b = (T.c1, T.xsq) if kind == "codes" else (T.p1, T.xsp)
+        o, i = a[:, C1 * k:C1 * k + C1], b[:, C1 * j:C1 * j + C1]
+        if kind == "codes": o, i = o.bitcast(U8), i.bitcast(U8)
+        es = near_eng if d in near else far_eng
+        g.remote_dma(o, i, T.sem["a1_%d" % k], T.sem.sent, pid, rid, bits(es))
+        count["sent"] = count.get("sent", 0) + len(es)
+
+    def fused(pairs, sem_of, engs):
+        ts = []
+        for (o, i, d), sm, es in zip(pairs, sem_of, engs):
+            rid, pid = to(d)
+            ts.append(RemoteDMATransfer(dst_ids=[DstId(rid=rid, pnc=pid)], dma_engine_mask=bits(es), remote_sem=T.sem[sm], src=i, dst=o))
+            count["sent"] = count.get("sent", 0) + len(es)
+        g.remote_dma_fused(ts, local_sem=T.sem.sent)
+
+    need("V", t_x, t_so)
+    need("S", t_x, t_so)
+    t_q = []
+    for j in range(3):
+        for t in (0, 1):
+            o, i = listed(j, t)
+            t_v = v(V.tensor_copy(out=o, in_=i))
+        for t in (2, 3):
+            o, i = listed(j, t)
+            t_s = s(S.activation(out=o, in_=i, func=COPY))
+        need("V", t_s, t_v)
+        t_q.append(v(V.quantize_mx(out=T.xsq[:, C1 * j:C1 * j + C1], scales=T.xsp[:, C1 * j:C1 * j + C1], in_=T.xs[:, 4 * C1 * j:4 * C1 * j + 4 * C1])))
+        if j == 0:
+            need("V", t_l)
+            t_a = v(V.tensor_copy(out=T.lf[:, :], in_=T.li[:, :]))
+            for q in range(4):
+                t_lc1 = v(V.tensor_copy(out=T.lc1[:, 32 * q:32 * q + 32], in_=T.l1[:, q:128:4]))
+            need("V", t_a)
+            t_lt = v(V.transpose(out=T.lt[:, :], in_=T.lf[:, :]))
+            need("V", t_ix)
+            t_ixc = v(V.tensor_scalar(out=T.ixc[0:96, :], in0=T.ix[0:96, :], scalar1=0.0, scalar2=None, op0=MAX))
+    need("g", t_q[0])
+    send1("codes", 0)
+    send1("planes", 0)
+    need("g", t_q[1])
+    send1("codes", 1)
+    need("g", t_q[2])
+    send1("codes", 2)
+    fused([(T.p1[:, C1 * slot(r, order[j]):C1 * slot(r, order[j]) + C1], T.xsp[:, C1 * j:C1 * j + C1], order[j]) for j in (1, 2)],
+          ["a1_%d" % slot(r, order[j]) for j in (1, 2)], [far_eng, near_eng])
+
+    need("Y", t_lt)
+    for hh in range(2):
+        for b in range(2):
+            n0 = 256 * hh + 128 * b
+            t_t4 = dma("d_t4", Y.dma_start(out=T.t4[n0:n0 + 128, :], in_=T.lt[:, 32 * b + 16 * hh:32 * b + 16 * hh + 16]))
+    need("Y", t_lc1)
+    for q in range(4):
+        t_d1 = dma("d_d1", Y.dma_start(out=T.d1[4 * q:4 * q + 4, :], in_=T.lc1[:, 32 * q:32 * q + 32]))
+    need("Y", t_d1)
+    for k in range(8):
+        t_e1 = dma("d_e1", Y.dma_start(out=T.e1[16 * k:16 * k + 16, :], in_=T.d1[:, :]))
+    need("g", t_t4, t_ixc)
+    for k in range(2):
+        t_i = dma("g_i", g.indirect_dma_start(out=T.cr[0:96, 4 * k:4 * k + 4], out_offset=None, in_=T.t4[:],
+                                              in_offset=IndirectOffsetOnAxis(ap=T.ixc[0:96, k:k + 1], axis=0), bounds_check=NODES - 1))
+
+    need("V", t_w1)
+    t_wq = v(V.quantize_mx(out=T.w1q[:, :], scales=T.w1p[:, :], in_=T.w1b[:, :]))
+    t_xq = v(V.quantize_mx(out=T.xq[:, :], scales=T.xp[:, :], in_=T.xb[:, :]))
+    need("V", t_l2)
+    for q in range(4):
+        t_lc2 = v(V.tensor_copy(out=T.lc2[:, 16 * q:16 * q + 16], in_=T.l2[:, q:64:4]))
+    need("V", t_w2)
+    t_w2q = v(V.quantize_mx(out=T.w2q[:, :], scales=T.w2p[:, :], in_=T.w2b[:, :]))
+    need("Y", t_lc2)
+    for q in range(4):
+        t_d2 = dma("d_d2", Y.dma_start(out=T.d2[4 * q:4 * q + 4, :], in_=T.lc2[:, 16 * q:16 * q + 16]))
+    need("Y", t_d2)
+    for k in range(8):
+        t_e2 = dma("d_e2", Y.dma_start(out=T.e2[16 * k:16 * k + 16, :], in_=T.d2[:, :]))
+    need("Y", t_i)
+    for k in range(8):
+        t_ec = dma("d_ec", Y.dma_start(out=T.ec[16 * k:16 * k + 16, :], in_=T.cr[0:96, :]))
+
+    free = {}
+    full = {}
+
+    def product(i, bank, rhs, plane, n):
+        if bank in free: need("P", free[bank])
+        return p(P.matmul_mx(T.ps[:, 512 * bank:512 * bank + n], T.w1q[:, 128 * i:128 * i + 128], T.w1p[:, 128 * i:128 * i + 128], rhs, plane, True, True))
+
+    def evacuate(i, bank, c0, n, tok):
+        src, dst = T.ps[:, 512 * bank:512 * bank + n], R[i][:, c0:c0 + n]
+        if i % 2 == 0:
+            need("V", tok)
+            full[i] = free[bank] = v(V.tensor_scalar(out=dst, in0=src, scalar1=0.0, scalar2=0.05, op0=MAX, op1=MULT))
+        else:
+            need("S", tok)
+            full[i] = free[bank] = s(S.activation(out=dst, in_=src, func=RELU, scale=0.05))
+
+    need("P", t_wq, t_xq)
+    toks = [product(i, i, T.xq[:, :], T.xp[:, :], NODES) for i in range(4)]
+    for i in range(4):
+        evacuate(i, i, 0, NODES, toks[i])
+    need("V", t_e1)
+    t_o1 = v(V.tensor_copy(out=T.o1[:, :], in_=T.e1[:, :]))
+    for a, sd in enumerate(arrive):
+        k = slot(sd, r)
+        es = near_eng if sd in near else far_eng
+        need("P", ("a1_%d" % k, 2 * len(es)))
+        b0 = 0 if a == 1 else 4
+        toks = [product(i, b0 + i, T.c1[:, C1 * k:C1 * k + C1], T.p1[:, C1 * k:C1 * k + C1], C1) for i in range(4)]
+        for i in range(4):
+            evacuate(i, b0 + i, NODES + C1 * sd, C1, toks[i])
+
+    def own(i, e, c0=0, c1=32): return R[i][:, 0:W1T].indirect(T.o1[:, 32 * e + c0:32 * e + c1])
+    def cmp(i, e): return R[i][:, 0:W1T].indirect(T.oc[:, 12 * e:12 * e + 12])
+
+    need("V", full[0], t_r)
+    need("S", full[0], t_r, t_o1)
+    need("V", t_o1)
+    t_v = v(V.tensor_copy(out=T.h[:, 0:1024:4], in_=own(0, 0, 0, 16)))
+    t_s = s(S.activation(out=T.h[:, 1024:2048:4], in_=own(0, 0, 16, 32), func=COPY))
+    need("S", full[1], full[2], full[3])
+    t_h1 = s(S.activation(out=T.h[:, 1:2048:4], in_=own(1, 0), func=COPY))
+    for e in range(2):
+        s(S.activation(out=T.bh[:, e:1536:3], in_=own(2, e), func=COPY))
+    tok = t_v
+    need("V", t_s)
+    for e in (1, 2, 3):
+        need("V", tok)
+        tok = v(V.tensor_tensor(out=T.h[:, 0:2048:4], in0=own(0, e), in1=T.h[:, 0:2048:4], op=MAX))
+    hdone = [tok]
+    need("V", t_ec)
+    for e in range(4):
+        t_oc = v(V.tensor_copy(out=T.oc[:, 12 * e:12 * e + 12], in_=T.ec[:, e:48:4]))
+    need("S", t_oc)
+    t_b = {}
+    for i in (1, 2, 3, 0):
+        for e in range(3):
+            t_b[i] = s(S.activation(out=T.bs[:, 576 * i + e:576 * i + 576:3], in_=cmp(i, e), func=COPY))
+    need("V", full[1], full[2], full[3])
+    tok = t_h1
+    for e in (1, 2, 3):
+        need("V", tok)
+        tok = v(V.tensor_tensor(out=T.h[:, 1:2048:4], in0=own(1, e), in1=T.h[:, 1:2048:4], op=MAX))
+    hdone.append(tok)
+    need("V", t_mask, t_oc)
+
+    def scan_l(i):
+        need("V", t_b[i])
+        return v(V.tensor_tensor_scan(T.bt[:, 576 * i:576 * i + 576], T.mask[:, 0:576], T.bs[:, 576 * i:576 * i + 576], 0.0, MULT, MAX))
+
+    def last_l(i, tok):
+        need("V", tok)
+        return v(V.tensor_tensor(out=T.hs[:, i:768:4], in0=cmp(i, 3), in1=T.bt[:, 576 * i + 2:576 * i + 576:3], op=MAX))
+    ta = scan_l(1)
+    tb = scan_l(2)
+    last_l(1, ta)
+    last_l(2, tb)
+    ta = scan_l(3)
+    tb = scan_l(0)
+    last_l(3, ta)
+    tok = last_l(0, tb)
+    need("V", tok)
+    t_hs = v(V.quantize_mx(out=T.hsq[:, :], scales=T.hsp[:, :], in_=T.hs[:, :]))
+
+    need("g", t_hs)
+    engs = {far[0]: far_eng[:half], far[1]: far_eng[half:], near[0]: near_eng}
+    cols = lambda a, k: a[:, C2 * k:C2 * k + C2]
+    fused([(cols(T.c2, slot(r, d)).bitcast(U8), cols(T.hsq, slot(d, r)).bitcast(U8), d) for d in order], ["a2"] * 3, [engs[d] for d in order])
+    fused([(cols(T.p2, slot(r, d)), cols(T.hsp, slot(d, r)), d) for d in order], ["a2"] * 3, [engs[d] for d in order])
+    t_a2 = ("a2", 2 * (half + (len(far_eng) - half) + len(near_eng)))
+
+    t_bh = {}
+    t_bh[2] = s(S.activation(out=T.bh[:, 2:1536:3], in_=own(2, 2), func=COPY))
+    for e in range(3):
+        t_bh[3] = s(S.activation(out=T.bh[:, 1536 + e:3072:3], in_=own(3, e), func=COPY))
+    need("V", t_e2)
+    t_o2 = v(V.tensor_copy(out=T.o2[:, :], in_=T.e2[:, :]))
+    for i in (2, 3):
+        b0 = 1536 * (i - 2)
+        need("V", t_bh[i])
+        tok = v(V.tensor_tensor_scan(T.bi[:, b0:b0 + 1536], T.mask[:, :], T.bh[:, b0:b0 + 1536], 0.0, MULT, MAX))
+        need("V", tok)
+        hdone.append(v(V.tensor_tensor(out=T.h[:, i:2048:4], in0=own(i, 3), in1=T.bi[:, b0 + 2:b0 + 1536:3], op=MAX)))
+
+    need("V", *hdone)
+    t_hq = [v(V.quantize_mx(out=T.hq[:, 256 * k:256 * k + 256], scales=T.hp[:, 256 * k:256 * k + 256], in_=T.h[:, 1024 * k:1024 * k + 1024])) for k in range(2)]
+
+    def product2(bank, rhs, plane, n):
+        need("P", free[bank])
+        return p(P.matmul_mx(T.ps[:, 512 * bank:512 * bank + n], T.w2q[:, :], T.w2p[:, :], rhs, plane, True, True))
+    need("P", t_w2q)
+    tu = []
+    for k in range(2):
+        need("P", t_hq[k])
+        tu.append(product2(k, T.hq[:, 256 * k:256 * k + 256], T.hp[:, 256 * k:256 * k + 256], 256))
+    need("P", t_a2)
+    tu.append(product2(2, T.c2[:, :], T.p2[:, :], 3 * C2))
+    need("S", tu[0])
+    t_s = s(S.activation(out=T.u[:, 0:256], in_=T.ps[:, 0:256], func=COPY))
+    need("V", tu[1])
+    t_v = v(V.tensor_copy(out=T.u[:, 256:512], in_=T.ps[:, 512:768]))
+    need("S", tu[2])
+    for d, n in runs:
+        k = slot(d, r)
+        t_s = s(S.activation(out=T.u[:, NODES + C2 * d:NODES + C2 * (d + n)], in_=T.ps[:, 1024 + C2 * k:1024 + C2 * (k + n)], func=COPY))
+
+    def tgt(e, c0=0, c1=16): return T.u[:, 0:W2T].indirect(T.o2[:, 16 * e + c0:16 * e + c1])
+    need("V", t_u, t_o2, t_s, t_v)
+    need("S", t_u, t_o2, t_s, t_v)
+    tok = v(V.tensor_copy(out=T.yb[:, 0:128], in_=tgt(0, 0, 8)))
+    t_s = s(S.activation(out=T.yb[:, 128:256], in_=tgt(0, 8, 16), func=COPY))
+    need("V", t_s)
+    for e in (1, 2, 3):
+        need("V", tok)
+        tok = v(V.tensor_tensor(out=T.yb[:, :], in0=tgt(e), in1=T.yb[:, :], op=MAX))
+    need("Y", tok)
+    t_y = dma("d_y", Y.dma_start(out=T.y[:, :], in_=T.yb[:, :]))
+
+    need("g", ("sent", count["sent"]))
+    need("Y", t_y, *[(k, count[k]) for k in ("cv", "cs", "ct")])

@@ -1,39 +1,38 @@
 import numpy as np
-from concourse.bass import DstId, RemoteDMATransfer, IndirectOffsetOnAxis
+from concourse.bass import DstId, RemoteDMATransfer
 from concourse.mybir import dt, AluOpType, ActivationFunctionType
 
 N, NODES, TG, C1, C2 = 4, 512, 256, 320, 64
 W1T = NODES + N * C1
 W2T = NODES + N * C2
 F8 = "float8_e4m3fn_x4"
+PW = 4 * C2
+HS = C1
+PLX = [0, C1 + 3 * C2, 2 * C1 + 3 * C2]
+BY, NAT, SN, SN4, OFW = 48, 192, 320, 332, 344
 SCRATCH = {
     "xb": ("sbuf", [128, 2048], "bfloat16"), "xq": ("sbuf", [128, 512], F8), "xp": ("sbuf", [128, 512], "uint8"),
     "w1b": ("sbuf", [128, 2048], "bfloat16"), "w1q": ("sbuf", [128, 512], F8), "w1p": ("sbuf", [128, 512], "uint8"),
     "w2b": ("sbuf", [128, 512], "bfloat16"), "w2q": ("sbuf", [128, 128], F8), "w2p": ("sbuf", [128, 128], "uint8"),
-    "xs": ("sbuf", [128, 12 * C1], "bfloat16"), "xsq": ("sbuf", [128, 3 * C1], F8), "xsp": ("sbuf", [128, 3 * C1], "uint8"),
+    "xs": ("sbuf", [128, 12 * C1], "bfloat16"), "xsq": ("sbuf", [128, 3 * C1], F8),
+    "hs": ("sbuf", [128, 12 * C2], "bfloat16"), "hsq": ("sbuf", [128, 3 * C2], F8),
+    "pl": ("sbuf", [128, 3 * C1 + 3 * C2], "uint8"),
     "c1": ("sbuf", [128, 3 * C1], F8), "p1": ("sbuf", [128, 3 * C1], "uint8"),
+    "c2": ("sbuf", [128, 2 * C2], F8), "p2": ("sbuf", [128, 2 * PW], "uint8"),
     "r0": ("sbuf", [128, W1T], "bfloat16"), "r1": ("sbuf", [128, W1T], "bfloat16"),
     "r2": ("sbuf", [128, W1T], "bfloat16"), "r3": ("sbuf", [128, W1T], "bfloat16"),
-    "h": ("sbuf", [128, 2048], "bfloat16"), "hq": ("sbuf", [128, 512], F8), "hp": ("sbuf", [128, 512], "uint8"),
-    "hs": ("sbuf", [128, 12 * C2], "bfloat16"), "hsq": ("sbuf", [128, 3 * C2], F8), "hsp": ("sbuf", [128, 3 * C2], "uint8"),
-    "c2": ("sbuf", [128, 3 * C2], F8), "p2": ("sbuf", [128, 3 * C2], "uint8"),
-    "mask": ("sbuf", [128, 1536], "bfloat16"),
-    "bs": ("sbuf", [128, 4 * 576], "bfloat16"), "bt": ("sbuf", [128, 4 * 576], "bfloat16"),
-    "bh": ("sbuf", [128, 2 * 1536], "bfloat16"), "bi": ("sbuf", [128, 2 * 1536], "bfloat16"),
+    "m0": ("sbuf", [128, 512], "bfloat16"), "m1": ("sbuf", [128, 512], "bfloat16"),
+    "a2": ("sbuf", [128, 2048], "bfloat16"), "a3": ("sbuf", [128, 2048], "bfloat16"),
+    "m2": ("sbuf", [128, 2048], "bfloat16"), "m3": ("sbuf", [128, 2048], "bfloat16"),
+    "mask": ("sbuf", [128, 1024], "bfloat16"),
+    "h": ("sbuf", [128, 2048], "bfloat16"), "hq": ("sbuf", [128, NODES + C2], F8), "hp": ("sbuf", [128, NODES + PW], "uint8"),
     "u": ("sbuf", [128, W2T], "float32"), "yb": ("sbuf", [128, TG], "float32"),
-    "sl": ("sbuf", [128, 80], "int32"), "sl4": ("sbuf", [128, 80], "int32"), "so": ("sbuf", [128, 320], "uint16"),
-    "l1": ("sbuf", [16, 128], "int32"), "lc1": ("sbuf", [16, 128], "int32"), "d1": ("dram", [16, 128], "int32"),
-    "e1": ("sbuf", [128, 128], "int32"), "o1": ("sbuf", [128, 128], "uint16"),
-    "l2": ("sbuf", [16, 64], "int32"), "lc2": ("sbuf", [16, 64], "int32"), "d2": ("dram", [16, 64], "int32"),
-    "e2": ("sbuf", [128, 64], "int32"), "o2": ("sbuf", [128, 64], "uint16"),
-    "li": ("sbuf", [32, 64], "int32"), "lf": ("sbuf", [32, 64], "float32"), "lt": ("sbuf", [32, 64], "float32"),
-    "t4": ("dram", [512, 4], "float32"),
-    "dsn": ("dram", [16, 12], "int32"), "ix": ("sbuf", [128, 2], "int32"), "ixc": ("sbuf", [128, 2], "int32"),
-    "cr": ("sbuf", [128, 8], "float32"), "ec": ("sbuf", [128, 48], "float32"), "oc": ("sbuf", [128, 48], "uint16"),
+    "sl": ("sbuf", [32, 80], "int32"), "sl4": ("sbuf", [128, 80], "int32"), "so": ("sbuf", [128, 320], "uint16"),
+    "ls": ("sbuf", [32, 192], "int32"), "lc": ("sbuf", [16, 192], "uint16"), "s2": ("sbuf", [32, 12], "int32"),
+    "s3": ("sbuf", [32, 12], "int32"), "of": ("sbuf", [128, OFW], "uint16"),
     "ps": ("psum", [128, 4096], "float32"),
 }
-SEMAPHORES = ["cv", "cs", "ct", "d_snd", "d_x", "g_l", "d_dsn", "d_ix", "d_l2", "d_w1", "d_w2", "d_t4", "d_d1", "d_e1",
-              "d_d2", "d_e2", "g_i", "d_ec", "d_y", "a1_0", "a1_1", "a1_2", "a2", "sent"]
+SEMAPHORES = ["cv", "cs", "ct", "d_snd", "d_ls", "d_x", "d_s2", "d_w1", "d_w2", "d_of", "d_y", "a1_0", "a1_1", "a1_2", "a2", "sent"]
 
 
 def rank_program(g, core, T, topo):
@@ -64,6 +63,10 @@ def rank_program(g, core, T, topo):
     def p(ins): return done("ct", ins)
     def dma(sem, ins): return done(sem, ins, 16)
 
+    def move(q, o, i, *toks):
+        need(q, *toks)
+        return v(V.tensor_copy(out=o, in_=i)) if q == "V" else s(S.activation(out=o, in_=i, func=COPY))
+
     others = [d for d in range(N) if d != r]
     me = T.cores[r]
     far = [d for d in others if topo.chip(T.cores[d]) != topo.chip(me)]
@@ -73,7 +76,6 @@ def rank_program(g, core, T, topo):
     arrive = [far[0], near[0], far[1]]
     far_eng = topo.engines(me, T.cores[far[0]])
     near_eng = [e for e in topo.engines(me, T.cores[near[0]]) if e not in far_eng]
-    half = len(far_eng) // 2
 
     def bits(es): return sum(1 << e for e in es)
     def slot(a, b): return a - (1 if a > b else 0)
@@ -82,24 +84,23 @@ def rank_program(g, core, T, topo):
         if runs and runs[-1][0] + runs[-1][1] == d: runs[-1][1] += 1
         else: runs.append([d, 1])
 
-    for k in range(4):
-        dma("d_snd", Y.dma_start(out=T.sl[16 * k:16 * k + 16, :], in_=T.snd1[:, :]))
-        t_snd = dma("d_snd", S.dma_start(out=T.sl[16 * (k + 4):16 * (k + 4) + 16, :], in_=T.snd1[:, :]))
-    dma("d_x", Y.dma_start(out=T.xb[:, 0:1024], in_=T.x[:, 0:1024]))
-    t_x = dma("d_x", S.dma_start(out=T.xb[:, 1024:2048], in_=T.x[:, 1024:2048]))
+    def pair(d):
+        return min(a for a in range(N - 1) if d not in (a, a + 1))
+
+    dma("d_snd", Y.dma_start(out=T.sl[0:16, :], in_=T.snd1[:, :]))
+    t_snd = dma("d_snd", S.dma_start(out=T.sl[16:32, :], in_=T.snd1[:, :]))
+    dma("d_ls", Y.dma_start(out=T.ls[0:16, 0:128], in_=T.src1[:, :]))
+    dma("d_ls", S.dma_start(out=T.ls[16:32, 0:128], in_=T.src1[:, :]))
+    t_ls = dma("d_ls", Y.dma_start(out=T.ls[0:16, 128:192], in_=T.src2[:, :]))
+    dma("d_x", S.dma_start(out=T.xb[:, 1024:2048], in_=T.x[:, 1024:2048]))
+    t_x = dma("d_x", Y.dma_start(out=T.xb[:, 0:1024], in_=T.x[:, 0:1024]))
+    t_w1 = dma("d_w1", Y.dma_start(out=T.w1b[:, :], in_=T.w1[:, :]))
     for k in range(2):
-        dma("g_l", g.dma_start(out=T.li[16 * k:16 * k + 16, :], in_=T.src1[:, 64 * k:64 * k + 64]))
-    t_l = dma("g_l", g.dma_start(out=T.l1[:, :], in_=T.src1[:, :]))
-    c = 0
-    for d, n in runs:
-        t_dsn = dma("d_dsn", Y.dma_start(out=T.dsn[:, c:c + 4 * n], in_=T.snd2[:, 4 * d:4 * d + 4 * n]))
-        c += 4 * n
-    dma("d_w1", Y.dma_start(out=T.w1b[:, 0:1024], in_=T.w1[:, 0:1024]))
-    t_w1 = dma("d_w1", S.dma_start(out=T.w1b[:, 1024:2048], in_=T.w1[:, 1024:2048]))
-    t_l2 = dma("d_l2", Y.dma_start(out=T.l2[:, :], in_=T.src2[:, :]))
+        c = 0
+        for d, n in runs:
+            t_s2 = dma("d_s2", Y.dma_start(out=T.s2[16 * k:16 * k + 16, c:c + 4 * n], in_=T.snd2[:, 4 * d:4 * d + 4 * n]))
+            c += 4 * n
     t_w2 = dma("d_w2", Y.dma_start(out=T.w2b[:, :], in_=T.w2[:, :]))
-    need("Y", t_dsn)
-    t_ix = dma("d_ix", Y.dma_start(out=T.ix[0:96, :], in_=T.dsn[:, :]))
 
     R = [T["r%d" % i] for i in range(4)]
     t_one = v(V.memset(T.mask[:, :], 1.0))
@@ -107,236 +108,183 @@ def rank_program(g, core, T, topo):
         t_r = v(V.memset(R[i][:, NODES + C1 * r:NODES + C1 * r + C1], 0.0))
     t_u = v(V.memset(T.u[:, NODES + C2 * r:NODES + C2 * r + C2], 0.0))
     need("V", t_one)
-    t_mask = v(V.memset(T.mask[:, 0::3], 0.0))
+    t_mask = v(V.memset(T.mask[:, 0::4], 0.0))
 
     need("V", t_snd)
-    t_a = v(V.tensor_scalar(out=T.sl4[:, :], in0=T.sl[:, :], scalar1=0.0, scalar2=4.0, op0=MAX, op1=MULT))
+    for k in range(4):
+        t_a = v(V.tensor_scalar(out=T.sl4[32 * k:32 * k + 32, :], in0=T.sl[:, :], scalar1=0.0, scalar2=4.0, op0=MAX, op1=MULT))
     need("V", t_a)
     for t in range(4):
         t_so = v(V.tensor_scalar(out=T.so[:, 80 * t:80 * t + 80], in0=T.sl4[:, :], scalar1=float(t), scalar2=None, op0=ADD))
+    need("V", t_ls)
+    for q in range(4):
+        t_lc = v(V.tensor_copy(out=T.lc[:, BY * q:BY * q + BY], in_=T.ls[0:16, q:192:4]))
+    v(V.tensor_copy(out=T.of[0:32, NAT:SN], in_=T.ls[:, 0:128]))
+    need("Y", t_lc)
+    for k in range(2):
+        for q in range(4):
+            t_of = dma("d_of", Y.dma_start(out=T.of[16 * k + 4 * q:16 * k + 4 * q + 4, 0:NAT], in_=T.lc[:, BY * q:BY * q + BY]))
 
-    def listed(j, t):
+    def listed(q, j, t):
         d = order[j]
-        return (T.xs[:, 4 * C1 * j + t:4 * C1 * (j + 1):4], T.xb[:, 0:2048].indirect(T.so[:, 80 * t + 20 * d:80 * t + 20 * d + 20]))
+        return move(q, T.xs[:, 4 * C1 * j + t:4 * C1 * (j + 1):4], T.xb[:, 0:2048].indirect(T.so[:, 80 * t + 20 * d:80 * t + 20 * d + 20]), t_x, t_so)
 
-    def to(d):
-        rid, pid, _ = topo.addr(T.cores[d])
-        return rid, pid
-
-    def send1(kind, j):
-        d = order[j]
-        k = slot(r, d)
-        rid, pid = to(d)
-        a, b = (T.c1, T.xsq) if kind == "codes" else (T.p1, T.xsp)
-        o, i = a[:, C1 * k:C1 * k + C1], b[:, C1 * j:C1 * j + C1]
-        if kind == "codes": o, i = o.bitcast(U8), i.bitcast(U8)
-        es = near_eng if d in near else far_eng
-        g.remote_dma(o, i, T.sem["a1_%d" % k], T.sem.sent, pid, rid, bits(es))
-        count["sent"] = count.get("sent", 0) + len(es)
-
-    def fused(pairs, sem_of, engs):
+    def send(parts):
         ts = []
-        for (o, i, d), sm, es in zip(pairs, sem_of, engs):
-            rid, pid = to(d)
+        for o, i, d, sm, es in parts:
+            rid, pid, _ = topo.addr(T.cores[d])
             ts.append(RemoteDMATransfer(dst_ids=[DstId(rid=rid, pnc=pid)], dma_engine_mask=bits(es), remote_sem=T.sem[sm], src=i, dst=o))
             count["sent"] = count.get("sent", 0) + len(es)
         g.remote_dma_fused(ts, local_sem=T.sem.sent)
 
-    need("V", t_x, t_so)
-    need("S", t_x, t_so)
-    t_q = []
-    for j in range(3):
-        for t in (0, 1):
-            o, i = listed(j, t)
-            t_v = v(V.tensor_copy(out=o, in_=i))
-        for t in (2, 3):
-            o, i = listed(j, t)
-            t_s = s(S.activation(out=o, in_=i, func=COPY))
-        need("V", t_s, t_v)
-        t_q.append(v(V.quantize_mx(out=T.xsq[:, C1 * j:C1 * j + C1], scales=T.xsp[:, C1 * j:C1 * j + C1], in_=T.xs[:, 4 * C1 * j:4 * C1 * j + 4 * C1])))
-        if j == 0:
-            need("V", t_l)
-            t_a = v(V.tensor_copy(out=T.lf[:, :], in_=T.li[:, :]))
-            for q in range(4):
-                t_lc1 = v(V.tensor_copy(out=T.lc1[:, 32 * q:32 * q + 32], in_=T.l1[:, q:128:4]))
-            need("V", t_a)
-            t_lt = v(V.transpose(out=T.lt[:, :], in_=T.lf[:, :]))
-            need("V", t_ix)
-            t_ixc = v(V.tensor_scalar(out=T.ixc[0:96, :], in0=T.ix[0:96, :], scalar1=0.0, scalar2=None, op0=MAX))
-    need("g", t_q[0])
-    send1("codes", 0)
-    send1("planes", 0)
-    need("g", t_q[1])
-    send1("codes", 1)
-    need("g", t_q[2])
-    send1("codes", 2)
-    fused([(T.p1[:, C1 * slot(r, order[j]):C1 * slot(r, order[j]) + C1], T.xsp[:, C1 * j:C1 * j + C1], order[j]) for j in (1, 2)],
-          ["a1_%d" % slot(r, order[j]) for j in (1, 2)], [far_eng, near_eng])
+    def part1(kind, j):
+        d = order[j]
+        k = slot(r, d)
+        if kind == "codes":
+            o, i = T.c1[:, C1 * k:C1 * k + C1].bitcast(U8), T.xsq[:, C1 * j:C1 * j + C1].bitcast(U8)
+        else:
+            o, i = T.p1[:, C1 * k:C1 * k + C1], T.pl[:, PLX[j]:PLX[j] + C1]
+        return (o, i, d, "a1_%d" % k, near_eng if d in near else far_eng)
 
-    need("Y", t_lt)
-    for hh in range(2):
-        for b in range(2):
-            n0 = 256 * hh + 128 * b
-            t_t4 = dma("d_t4", Y.dma_start(out=T.t4[n0:n0 + 128, :], in_=T.lt[:, 32 * b + 16 * hh:32 * b + 16 * hh + 16]))
-    need("Y", t_lc1)
-    for q in range(4):
-        t_d1 = dma("d_d1", Y.dma_start(out=T.d1[4 * q:4 * q + 4, :], in_=T.lc1[:, 32 * q:32 * q + 32]))
-    need("Y", t_d1)
-    for k in range(8):
-        t_e1 = dma("d_e1", Y.dma_start(out=T.e1[16 * k:16 * k + 16, :], in_=T.d1[:, :]))
-    need("g", t_t4, t_ixc)
-    for k in range(2):
-        t_i = dma("g_i", g.indirect_dma_start(out=T.cr[0:96, 4 * k:4 * k + 4], out_offset=None, in_=T.t4[:],
-                                              in_offset=IndirectOffsetOnAxis(ap=T.ixc[0:96, k:k + 1], axis=0), bounds_check=NODES - 1))
+    t_q = []
+    for j, share in enumerate(("VVSS", "VVSS", "VSSS")):
+        toks = [listed(q, j, t) for t, q in enumerate(share)]
+        need("V", *toks)
+        t_q.append(v(V.quantize_mx(out=T.xsq[:, C1 * j:C1 * j + C1], scales=T.pl[:, PLX[j]:PLX[j] + C1], in_=T.xs[:, 4 * C1 * j:4 * C1 * j + 4 * C1])))
+    need("g", t_q[0])
+    send([part1("codes", 0)])
+    send([part1("planes", 0)])
+    need("g", t_q[2])
+    send([part1("codes", 1), part1("codes", 2)])
+    send([part1("planes", 1), part1("planes", 2)])
 
     need("V", t_w1)
-    t_wq = v(V.quantize_mx(out=T.w1q[:, :], scales=T.w1p[:, :], in_=T.w1b[:, :]))
     t_xq = v(V.quantize_mx(out=T.xq[:, :], scales=T.xp[:, :], in_=T.xb[:, :]))
-    need("V", t_l2)
-    for q in range(4):
-        t_lc2 = v(V.tensor_copy(out=T.lc2[:, 16 * q:16 * q + 16], in_=T.l2[:, q:64:4]))
+    t_wq = [v(V.quantize_mx(out=T.w1q[:, 256 * k:256 * k + 256], scales=T.w1p[:, 256 * k:256 * k + 256], in_=T.w1b[:, 1024 * k:1024 * k + 1024])) for k in range(2)]
+    need("V", t_s2)
+    v(V.tensor_copy(out=T.of[0:32, SN:SN4], in_=T.s2[:, :]))
+    t_a = v(V.tensor_scalar(out=T.s3[:, :], in0=T.s2[:, :], scalar1=4.0, scalar2=3.0, op0=MULT, op1=ADD))
     need("V", t_w2)
     t_w2q = v(V.quantize_mx(out=T.w2q[:, :], scales=T.w2p[:, :], in_=T.w2b[:, :]))
-    need("Y", t_lc2)
-    for q in range(4):
-        t_d2 = dma("d_d2", Y.dma_start(out=T.d2[4 * q:4 * q + 4, :], in_=T.lc2[:, 16 * q:16 * q + 16]))
-    need("Y", t_d2)
-    for k in range(8):
-        t_e2 = dma("d_e2", Y.dma_start(out=T.e2[16 * k:16 * k + 16, :], in_=T.d2[:, :]))
-    need("Y", t_i)
-    for k in range(8):
-        t_ec = dma("d_ec", Y.dma_start(out=T.ec[16 * k:16 * k + 16, :], in_=T.cr[0:96, :]))
+    need("V", t_a)
+    t_a = v(V.tensor_copy(out=T.of[0:32, SN4:OFW], in_=T.s3[:, :]))
+    need("V", t_a, t_of)
+    for k in (1, 2, 3):
+        t_off = v(V.tensor_copy(out=T.of[32 * k:32 * k + 32, :], in_=T.of[0:32, :]))
 
     free = {}
     full = {}
 
     def product(i, bank, rhs, plane, n):
+        need("P", t_wq[i // 2])
         if bank in free: need("P", free[bank])
         return p(P.matmul_mx(T.ps[:, 512 * bank:512 * bank + n], T.w1q[:, 128 * i:128 * i + 128], T.w1p[:, 128 * i:128 * i + 128], rhs, plane, True, True))
 
-    def evacuate(i, bank, c0, n, tok):
+    def evacuate(q, i, bank, c0, n, tok):
         src, dst = T.ps[:, 512 * bank:512 * bank + n], R[i][:, c0:c0 + n]
-        if i % 2 == 0:
-            need("V", tok)
-            full[i] = free[bank] = v(V.tensor_scalar(out=dst, in0=src, scalar1=0.0, scalar2=0.05, op0=MAX, op1=MULT))
+        need(q, tok)
+        if q == "V":
+            free[bank] = v(V.tensor_scalar(out=dst, in0=src, scalar1=0.0, scalar2=0.05, op0=MAX, op1=MULT))
         else:
-            need("S", tok)
-            full[i] = free[bank] = s(S.activation(out=dst, in_=src, func=RELU, scale=0.05))
+            free[bank] = s(S.activation(out=dst, in_=src, func=RELU, scale=0.05))
+        full.setdefault(i, []).append(free[bank])
 
-    need("P", t_wq, t_xq)
+    need("P", t_xq)
     toks = [product(i, i, T.xq[:, :], T.xp[:, :], NODES) for i in range(4)]
-    for i in range(4):
-        evacuate(i, i, 0, NODES, toks[i])
-    need("V", t_e1)
-    t_o1 = v(V.tensor_copy(out=T.o1[:, :], in_=T.e1[:, :]))
+    for i, q in enumerate("SSSV"):
+        evacuate(q, i, i, 0, NODES, toks[i])
     for a, sd in enumerate(arrive):
         k = slot(sd, r)
         es = near_eng if sd in near else far_eng
         need("P", ("a1_%d" % k, 2 * len(es)))
         b0 = 0 if a == 1 else 4
         toks = [product(i, b0 + i, T.c1[:, C1 * k:C1 * k + C1], T.p1[:, C1 * k:C1 * k + C1], C1) for i in range(4)]
-        for i in range(4):
-            evacuate(i, b0 + i, NODES + C1 * sd, C1, toks[i])
+        for i, q in enumerate("SVVV" if a == 2 else "SVSV"):
+            evacuate(q, i, b0 + i, NODES + C1 * sd, C1, toks[i])
 
-    def own(i, e, c0=0, c1=32): return R[i][:, 0:W1T].indirect(T.o1[:, 32 * e + c0:32 * e + c1])
-    def cmp(i, e): return R[i][:, 0:W1T].indirect(T.oc[:, 12 * e:12 * e + 12])
+    M = [T["m%d" % i] for i in range(4)]
+    A = {2: T.a2, 3: T.a3}
+    last = {}
 
-    need("V", full[0], t_r)
-    need("S", full[0], t_r, t_o1)
-    need("V", t_o1)
-    t_v = v(V.tensor_copy(out=T.h[:, 0:1024:4], in_=own(0, 0, 0, 16)))
-    t_s = s(S.activation(out=T.h[:, 1024:2048:4], in_=own(0, 0, 16, 32), func=COPY))
-    need("S", full[1], full[2], full[3])
-    t_h1 = s(S.activation(out=T.h[:, 1:2048:4], in_=own(1, 0), func=COPY))
-    for e in range(2):
-        s(S.activation(out=T.bh[:, e:1536:3], in_=own(2, e), func=COPY))
-    tok = t_v
-    need("V", t_s)
-    for e in (1, 2, 3):
-        need("V", tok)
-        tok = v(V.tensor_tensor(out=T.h[:, 0:2048:4], in0=own(0, e), in1=T.h[:, 0:2048:4], op=MAX))
-    hdone = [tok]
-    need("V", t_ec)
-    for e in range(4):
-        t_oc = v(V.tensor_copy(out=T.oc[:, 12 * e:12 * e + 12], in_=T.ec[:, e:48:4]))
-    need("S", t_oc)
-    t_b = {}
-    for i in (1, 2, 3, 0):
-        for e in range(3):
-            t_b[i] = s(S.activation(out=T.bs[:, 576 * i + e:576 * i + 576:3], in_=cmp(i, e), func=COPY))
-    need("V", full[1], full[2], full[3])
-    tok = t_h1
-    for e in (1, 2, 3):
-        need("V", tok)
-        tok = v(V.tensor_tensor(out=T.h[:, 1:2048:4], in0=own(1, e), in1=T.h[:, 1:2048:4], op=MAX))
-    hdone.append(tok)
-    need("V", t_mask, t_oc)
+    def src(i, e, n0, n1): return R[i][:, 0:W1T].indirect(T.of[:, BY * e + n0 // 16:BY * e + n1 // 16])
 
-    def scan_l(i):
-        need("V", t_b[i])
-        return v(V.tensor_tensor_scan(T.bt[:, 576 * i:576 * i + 576], T.mask[:, 0:576], T.bs[:, 576 * i:576 * i + 576], 0.0, MULT, MAX))
+    def first(i, n0, n1):
+        last[i, n0] = move("S", M[i][:, n0:n1], src(i, 0, n0, n1), t_off, t_r, *full[i])
 
-    def last_l(i, tok):
-        need("V", tok)
-        return v(V.tensor_tensor(out=T.hs[:, i:768:4], in0=cmp(i, 3), in1=T.bt[:, 576 * i + 2:576 * i + 576:3], op=MAX))
-    ta = scan_l(1)
-    tb = scan_l(2)
-    last_l(1, ta)
-    last_l(2, tb)
-    ta = scan_l(3)
-    tb = scan_l(0)
-    last_l(3, ta)
-    tok = last_l(0, tb)
-    need("V", tok)
-    t_hs = v(V.quantize_mx(out=T.hsq[:, :], scales=T.hsp[:, :], in_=T.hs[:, :]))
+    def more(i, e, n0, n1):
+        need("V", last[i, n0], *full[i])
+        last[i, n0] = v(V.tensor_tensor(out=M[i][:, n0:n1], in0=src(i, e, n0, n1), in1=M[i][:, n0:n1], op=MAX))
 
-    need("g", t_hs)
-    engs = {far[0]: far_eng[:half], far[1]: far_eng[half:], near[0]: near_eng}
-    cols = lambda a, k: a[:, C2 * k:C2 * k + C2]
-    fused([(cols(T.c2, slot(r, d)).bitcast(U8), cols(T.hsq, slot(d, r)).bitcast(U8), d) for d in order], ["a2"] * 3, [engs[d] for d in order])
-    fused([(cols(T.p2, slot(r, d)), cols(T.hsp, slot(d, r)), d) for d in order], ["a2"] * 3, [engs[d] for d in order])
-    t_a2 = ("a2", 2 * (half + (len(far_eng) - half) + len(near_eng)))
+    def four(i, n0, n1):
+        last[i, n0] = move("S", A[i][:, 4 * n0:4 * n1], R[i][:, 0:W1T].indirect(T.of[:, NAT + n0 // 4:NAT + n1 // 4]), t_off, t_r, *full[i])
 
-    t_bh = {}
-    t_bh[2] = s(S.activation(out=T.bh[:, 2:1536:3], in_=own(2, 2), func=COPY))
-    for e in range(3):
-        t_bh[3] = s(S.activation(out=T.bh[:, 1536 + e:3072:3], in_=own(3, e), func=COPY))
-    need("V", t_e2)
-    t_o2 = v(V.tensor_copy(out=T.o2[:, :], in_=T.e2[:, :]))
-    for i in (2, 3):
-        b0 = 1536 * (i - 2)
-        need("V", t_bh[i])
-        tok = v(V.tensor_tensor_scan(T.bi[:, b0:b0 + 1536], T.mask[:, :], T.bh[:, b0:b0 + 1536], 0.0, MULT, MAX))
-        need("V", tok)
-        hdone.append(v(V.tensor_tensor(out=T.h[:, i:2048:4], in0=own(i, 3), in1=T.bi[:, b0 + 2:b0 + 1536:3], op=MAX)))
+    def scan(i, n0, n1):
+        need("V", last[i, n0], t_mask)
+        last[i, n0] = v(V.tensor_tensor_scan(M[i][:, 4 * n0:4 * n1], T.mask[:, 0:4 * (n1 - n0)], A[i][:, 4 * n0:4 * n1], 0.0, MULT, MAX))
 
-    need("V", *hdone)
-    t_hq = [v(V.quantize_mx(out=T.hq[:, 256 * k:256 * k + 256], scales=T.hp[:, 256 * k:256 * k + 256], in_=T.h[:, 1024 * k:1024 * k + 1024])) for k in range(2)]
+    def table(i): return [t for (a, _), t in last.items() if a == i]
+
+    def slots(q, i):
+        win, c = (M[i][:, 0:512], SN) if i < 2 else (M[i][:, 0:2048], SN4)
+        return move(q, T.hs[:, i:768:4], win.indirect(T.of[:, c:c + 12]), *table(i))
+
+    first(0, 0, 256); first(0, 256, 512); first(1, 0, 512)
+    four(2, 0, 256); four(2, 256, 512); four(3, 0, 256); four(3, 256, 384); four(3, 384, 512)
+    need("V", t_off)
+    more(0, 1, 0, 256); more(0, 1, 256, 512); more(0, 2, 0, 256)
+    more(1, 1, 0, 512); more(0, 2, 256, 512); more(0, 3, 0, 256)
+    scan(2, 0, 256); more(0, 3, 256, 512); more(1, 2, 0, 512)
+    scan(2, 256, 512); more(1, 3, 0, 512)
+    t_hs = [slots("V", 0)]
+    scan(3, 0, 256)
+    t_hs.append(slots("V", 1))
+    scan(3, 256, 384); scan(3, 384, 512)
+    t_hs.append(slots("S", 2))
+    t_hs.append(slots("V", 3))
+    need("V", *t_hs)
+    t_hq = v(V.quantize_mx(out=T.hsq[:, :], scales=T.pl[:, HS:HS + 3 * C2], in_=T.hs[:, :]))
+
+    need("g", t_hq)
+    parts = []
+    quarter, half = len(far_eng) // 4, len(near_eng) // 2
+    engs = {far[0]: (far_eng[:quarter], far_eng[quarter:2 * quarter]), far[1]: (far_eng[2 * quarter:3 * quarter], far_eng[3 * quarter:]),
+            near[0]: (near_eng[:half], near_eng[half:])}
+    for d in order:
+        c0 = C2 * slot(d, r)
+        a = r - pair(d)
+        codes = T.c2[:, C2 * a:C2 * a + C2] if a in (0, 1) else T.hq[:, NODES:NODES + C2]
+        plane = T.p2[:, PW * a:PW * a + PW] if a in (0, 1) else T.hp[:, NODES:NODES + PW]
+        w0 = HS + c0 - (PW - C2 if a == 0 else 0)
+        parts.append((codes.bitcast(U8), T.hsq[:, c0:c0 + C2].bitcast(U8), d, "a2", engs[d][0]))
+        parts.append((plane, T.pl[:, w0:w0 + PW], d, "a2", engs[d][1]))
+    send(parts)
+    t_a2 = ("a2", len(far_eng) + len(near_eng))
 
     def product2(bank, rhs, plane, n):
         need("P", free[bank])
         return p(P.matmul_mx(T.ps[:, 512 * bank:512 * bank + n], T.w2q[:, :], T.w2p[:, :], rhs, plane, True, True))
     need("P", t_w2q)
-    tu = []
-    for k in range(2):
-        need("P", t_hq[k])
-        tu.append(product2(k, T.hq[:, 256 * k:256 * k + 256], T.hp[:, 256 * k:256 * k + 256], 256))
+    toks = []
+    for i, q in enumerate("VVVS"):
+        toks.append(move(q, T.h[:, i:2048:4], M[i][:, :] if i < 2 else M[i][:, 3:2048:4], *table(i)))
+    need("V", *toks)
+    t_own = []
+    for k, q in enumerate("SV"):
+        t_h = v(V.quantize_mx(out=T.hq[:, 256 * k:256 * k + 256], scales=T.hp[:, 256 * k:256 * k + 256], in_=T.h[:, 1024 * k:1024 * k + 1024]))
+        need("P", t_h)
+        t_own.append(product2(k, T.hq[:, 256 * k:256 * k + 256], T.hp[:, 256 * k:256 * k + 256], 256))
+    t_tab = [move(q, T.u[:, 256 * k:256 * k + 256], T.ps[:, 512 * k:512 * k + 256], t_own[k]) for k, q in enumerate("SV")]
     need("P", t_a2)
-    tu.append(product2(2, T.c2[:, :], T.p2[:, :], 3 * C2))
-    need("S", tu[0])
-    t_s = s(S.activation(out=T.u[:, 0:256], in_=T.ps[:, 0:256], func=COPY))
-    need("V", tu[1])
-    t_v = v(V.tensor_copy(out=T.u[:, 256:512], in_=T.ps[:, 512:768]))
-    need("S", tu[2])
-    for d, n in runs:
-        k = slot(d, r)
-        t_s = s(S.activation(out=T.u[:, NODES + C2 * d:NODES + C2 * (d + n)], in_=T.ps[:, 1024 + C2 * k:1024 + C2 * (k + n)], func=COPY))
+    ta = product2(2, T.c2[:, :], T.p2[:, PW - C2:PW + C2], 2 * C2)
+    tb = product2(3, T.hq[:, NODES - C2:NODES + C2], T.hp[:, NODES - C2:NODES + C2], 2 * C2)
+    a = pair(r)
+    b = [d for d in others if d not in (a, a + 1)][0]
+    t_tab.append(move("V", T.u[:, NODES + C2 * a:NODES + C2 * (a + 2)], T.ps[:, 1024:1024 + 2 * C2], ta))
+    t_tab.append(move("S", T.u[:, NODES + C2 * b:NODES + C2 * (b + 1)], T.ps[:, 1536 + C2:1536 + 2 * C2], tb))
 
-    def tgt(e, c0=0, c1=16): return T.u[:, 0:W2T].indirect(T.o2[:, 16 * e + c0:16 * e + c1])
-    need("V", t_u, t_o2, t_s, t_v)
-    need("S", t_u, t_o2, t_s, t_v)
-    tok = v(V.tensor_copy(out=T.yb[:, 0:128], in_=tgt(0, 0, 8)))
-    t_s = s(S.activation(out=T.yb[:, 128:256], in_=tgt(0, 8, 16), func=COPY))
+    def tgt(e, c0=0, c1=16): return T.u[:, 0:W2T].indirect(T.of[:, BY * e + 32 + c0:BY * e + 32 + c1])
+    tok = move("V", T.yb[:, 0:128], tgt(0, 0, 8), t_u, *t_tab)
+    t_s = move("S", T.yb[:, 128:256], tgt(0, 8, 16), t_u, *t_tab)
     need("V", t_s)
     for e in (1, 2, 3):
         need("V", tok)

@@ -7,9 +7,8 @@ W1T = NODES + N * C1
 W2T = NODES + N * C2
 F8 = "float8_e4m3fn_x4"
 PW = 4 * C2
-HS = C1
-PLX = [0, C1 + 3 * C2, 2 * C1 + 3 * C2]
-BY, NAT, SN, SN4, OFW = 48, 192, 320, 332, 344
+BY, NAT, SN, SN4, OC, OFW = 48, 192, 320, 332, 360, 408
+H0 = 16
 SCRATCH = {
     "xb": ("sbuf", [128, 2048], "bfloat16"), "xq": ("sbuf", [128, 512], F8), "xp": ("sbuf", [128, 512], "uint8"),
     "w1b": ("sbuf", [128, 2048], "bfloat16"), "w1q": ("sbuf", [128, 512], F8), "w1p": ("sbuf", [128, 512], "uint8"),
@@ -17,7 +16,7 @@ SCRATCH = {
     "xs": ("sbuf", [128, 12 * C1], "bfloat16"), "xsq": ("sbuf", [128, 3 * C1], F8),
     "hs": ("sbuf", [128, 12 * C2], "bfloat16"), "hsq": ("sbuf", [128, 3 * C2], F8),
     "pl": ("sbuf", [128, 3 * C1 + 3 * C2], "uint8"),
-    "c1": ("sbuf", [128, 3 * C1], F8), "p1": ("sbuf", [128, 3 * C1], "uint8"),
+    "c1": ("sbuf", [128, 3 * C1], F8), "p1": ("sbuf", [128, 4 * NODES], "uint8"),
     "c2": ("sbuf", [128, 2 * C2], F8), "p2": ("sbuf", [128, 2 * PW], "uint8"),
     "r0": ("sbuf", [128, W1T], "bfloat16"), "r1": ("sbuf", [128, W1T], "bfloat16"),
     "r2": ("sbuf", [128, W1T], "bfloat16"), "r3": ("sbuf", [128, W1T], "bfloat16"),
@@ -25,14 +24,28 @@ SCRATCH = {
     "a2": ("sbuf", [128, 2048], "bfloat16"), "a3": ("sbuf", [128, 2048], "bfloat16"),
     "m2": ("sbuf", [128, 2048], "bfloat16"), "m3": ("sbuf", [128, 2048], "bfloat16"),
     "mask": ("sbuf", [128, 1024], "bfloat16"),
-    "h": ("sbuf", [128, 2048], "bfloat16"), "hq": ("sbuf", [128, NODES + C2], F8), "hp": ("sbuf", [128, NODES + PW], "uint8"),
+    "h": ("sbuf", [128, 2064], "bfloat16"), "hq": ("sbuf", [128, NODES + C2], F8), "hp": ("sbuf", [128, NODES + PW], "uint8"),
     "u": ("sbuf", [128, W2T], "float32"), "yb": ("sbuf", [128, TG], "float32"),
-    "sl": ("sbuf", [32, 80], "int32"), "sl4": ("sbuf", [128, 80], "int32"), "so": ("sbuf", [128, 320], "uint16"),
-    "ls": ("sbuf", [32, 192], "int32"), "lc": ("sbuf", [16, 192], "uint16"), "s2": ("sbuf", [32, 12], "int32"),
-    "s3": ("sbuf", [32, 12], "int32"), "of": ("sbuf", [128, OFW], "uint16"),
+    "sl": ("sbuf", [128, 80], "int32"), "so": ("sbuf", [128, 320], "uint16"),
+    "ls": ("sbuf", [32, 204], "int32"), "lc": ("sbuf", [16, 192], "uint16"),
+    "of": ("sbuf", [128, OFW], "uint16"),
+    "s4": ("sbuf", [32, 12], "int32"), "k1": ("sbuf", [32, 12], "int32"), "k2": ("sbuf", [32, 12], "float32"),
+    "k3": ("sbuf", [32, 12], "float32"), "ko": ("sbuf", [128, 12], "uint16"), "bye": ("sbuf", [128, 512], "int32"),
+    "ga": ("sbuf", [128, 192], "float32"), "gt": ("sbuf", [32, 192], "float32"), "oc": ("sbuf", [16, 48], "uint16"),
+    "b1": ("sbuf", [128, 2, 192], "bfloat16"), "b4": ("sbuf", [128, 768], "bfloat16"),
     "ps": ("psum", [128, 4096], "float32"),
 }
-SEMAPHORES = ["cv", "cs", "ct", "d_snd", "d_ls", "d_x", "d_s2", "d_w1", "d_w2", "d_of", "d_y", "a1_0", "a1_1", "a1_2", "a2", "sent"]
+SEMAPHORES = ["cg", "cv", "cs", "ct", "d_snd", "d_ls", "d_x", "d_s2", "d_w1", "d_w2", "d_of", "d_off", "d_bye", "d_s4", "d_oc", "d_y",
+              "a1_0", "a1_1", "a1_2", "a1_3", "a2", "sent"]
+CFG = dict(
+    pieces={"A": (0, 0, 128), "B": (0, 128, 320), "C": (2, 0, 192), "D": (2, 192, 320)},
+    deliv=[(0, 0, 320, 320), (2, 0, 192, 320), (1, 0, 320, 320), (2, 192, 320, 512)], pl=(640, [0, 832, 320]),
+    front="AVVSS K0 qA BVVSS K1 qB CVSSS K23 qC X 1VSSS W0 k1 q1 DVSSS k2 W1 qD L", calls="cAf cBf+cCn paf+pbn c1f pcf cDm+pdk", repdma=True,
+    mm="o0 o1 o2 o3 a0 a1 a2 a3 b0 b1 b2 b3 c0 c1 d0 d1 c2 d2 c3 d3",
+    work="k3 o0S o1V k4 o2S o3V k5 a0S a1V k6 a2S a3V k7 b0S b1S b2S b3S c0V d0V c1V d1V "
+         "f0 c2V d2V f1 g2a g2b c3S d3V N g3e m01 m11 m02 m12 z2a z2b M03a M13 M03b Z U T HV0 HS1 HV2 "
+         "g3f g3c g3d Q s3e s3f s3c iV3a s3d ha iS3c hc iV3d hd uVa uSc uVd",
+    inter="SSVV", ycuts=[("V", 0, 6), ("S", 6, 16)], yorder="01 11 02 12 03 13", ystore=[("Y", 0, 6), ("S", 6, 16)], xfirst=True, sndn=2, waw=True)
 
 
 def rank_program(g, core, T, topo):
@@ -73,7 +86,6 @@ def rank_program(g, core, T, topo):
     far.sort(key=lambda d: topo.die(T.cores[d]) != topo.die(me))
     near = [d for d in others if d not in far]
     order = [far[0], far[1], near[0]]
-    arrive = [far[0], near[0], far[1]]
     far_eng = topo.engines(me, T.cores[far[0]])
     near_eng = [e for e in topo.engines(me, T.cores[near[0]]) if e not in far_eng]
 
@@ -87,47 +99,75 @@ def rank_program(g, core, T, topo):
     def pair(d):
         return min(a for a in range(N - 1) if d not in (a, a + 1))
 
-    dma("d_snd", Y.dma_start(out=T.sl[0:16, :], in_=T.snd1[:, :]))
-    t_snd = dma("d_snd", S.dma_start(out=T.sl[16:32, :], in_=T.snd1[:, :]))
-    dma("d_ls", Y.dma_start(out=T.ls[0:16, 0:128], in_=T.src1[:, :]))
-    dma("d_ls", S.dma_start(out=T.ls[16:32, 0:128], in_=T.src1[:, :]))
-    t_ls = dma("d_ls", Y.dma_start(out=T.ls[0:16, 128:192], in_=T.src2[:, :]))
-    dma("d_x", S.dma_start(out=T.xb[:, 1024:2048], in_=T.x[:, 1024:2048]))
-    t_x = dma("d_x", Y.dma_start(out=T.xb[:, 0:1024], in_=T.x[:, 0:1024]))
-    t_w1 = dma("d_w1", Y.dma_start(out=T.w1b[:, :], in_=T.w1[:, :]))
+    SG = CFG["sndn"]
+    for k in range(SG):
+        t_snd = dma("d_snd", (Y, S)[k % 2].dma_start(out=T.sl[16 * k:16 * k + 16, :], in_=T.snd1[:, :]))
+    for w in ("xl" if CFG["xfirst"] else "lx"):
+        if w == "l":
+            dma("d_ls", Y.dma_start(out=T.ls[0:16, 64:192], in_=T.src1[:, :]))
+            t_ls = dma("d_ls", S.dma_start(out=T.ls[0:16, 0:64], in_=T.src2[:, :]))
+        else:
+            dma("d_x", S.dma_start(out=T.xb[64:128, :], in_=T.x[64:128, :]))
+            t_x = dma("d_x", Y.dma_start(out=T.xb[0:64, :], in_=T.x[0:64, :]))
+    dma("d_s2", S.dma_start(out=T.ls[16:32, 64:192], in_=T.src1[:, :]))
     for k in range(2):
-        c = 0
+        c = 192
         for d, n in runs:
-            t_s2 = dma("d_s2", Y.dma_start(out=T.s2[16 * k:16 * k + 16, c:c + 4 * n], in_=T.snd2[:, 4 * d:4 * d + 4 * n]))
+            t_s2 = dma("d_s2", (Y, S)[k].dma_start(out=T.ls[16 * k:16 * k + 16, c:c + 4 * n], in_=T.snd2[:, 4 * d:4 * d + 4 * n]))
             c += 4 * n
+    t_w1 = dma("d_w1", Y.dma_start(out=T.w1b[:, :], in_=T.w1[:, :]))
     t_w2 = dma("d_w2", Y.dma_start(out=T.w2b[:, :], in_=T.w2[:, :]))
 
     R = [T["r%d" % i] for i in range(4)]
+    if "k7" in CFG["work"]:
+        t_s4 = v(V.memset(T.s4[:, :], 0))
+        t_ko = v(V.memset(T.ko[:, :], 0))
     t_one = v(V.memset(T.mask[:, :], 1.0))
     for i in range(4):
         t_r = v(V.memset(R[i][:, NODES + C1 * r:NODES + C1 * r + C1], 0.0))
-    t_u = v(V.memset(T.u[:, NODES + C2 * r:NODES + C2 * r + C2], 0.0))
-    need("V", t_one)
-    t_mask = v(V.memset(T.mask[:, 0::4], 0.0))
+
+    if "k7" in CFG["work"]:
+        t_bye = done("cg", g.iota(T.bye[:, :], [[0, 512]], 0, 0))
+        need("Y", t_bye, t_s4, t_ko)
+        for k in range(2):
+            for a in range(4):
+                t_bye = dma("d_bye", Y.dma_start(out=T.bye[16 * k:16 * k + 4, 128 * a:128 * a + 128], in_=T.src1[4 * a:4 * a + 4, :]))
+            c = 0
+            for d, n in runs:
+                c0 = k if c == 0 else 0
+                t_s4 = dma("d_s4", Y.dma_start(out=T.s4[16 * k:16 * k + 16, c + c0 - k:c + 4 * n - k], in_=T.snd2[:, 4 * d + c0:4 * d + 4 * n]))
+                c += 4 * n
+    t_m2 = done("cg", g.iota(T.m2[:, 0:1024], [[0, 1024]], 0, 0, allow_small_or_imprecise_dtypes=True)) if "f2" in CFG["work"] else t_r
 
     need("V", t_snd)
-    for k in range(4):
-        t_a = v(V.tensor_scalar(out=T.sl4[32 * k:32 * k + 32, :], in0=T.sl[:, :], scalar1=0.0, scalar2=4.0, op0=MAX, op1=MULT))
-    need("V", t_a)
-    for t in range(4):
-        t_so = v(V.tensor_scalar(out=T.so[:, 80 * t:80 * t + 80], in0=T.sl4[:, :], scalar1=float(t), scalar2=None, op0=ADD))
-    need("V", t_ls)
-    for q in range(4):
-        t_lc = v(V.tensor_copy(out=T.lc[:, BY * q:BY * q + BY], in_=T.ls[0:16, q:192:4]))
-    v(V.tensor_copy(out=T.of[0:32, NAT:SN], in_=T.ls[:, 0:128]))
-    need("Y", t_lc)
-    for k in range(2):
-        for q in range(4):
-            t_of = dma("d_of", Y.dma_start(out=T.of[16 * k + 4 * q:16 * k + 4 * q + 4, 0:NAT], in_=T.lc[:, BY * q:BY * q + BY]))
+    for k in range(16 * SG, 128, 16 * SG):
+        t_a = v(V.tensor_copy(out=T.sl[k:k + 16 * SG, :], in_=T.sl[0:16 * SG, :]))
+    need("V", t_one)
+    t_mask = v(V.memset(T.mask[:, 0::4], 0.0))
+    if SG < 8: need("V", t_a)
+    t_so = {}
+    for t in (2, 0, 3, 1):
+        t_so[t] = v(V.tensor_scalar(out=T.so[:, 80 * t:80 * t + 80], in0=T.sl[:, :], scalar1=4.0, scalar2=float(t), op0=MULT, op1=ADD))
+    if " H" in CFG["work"]:
+        t_h0 = v(V.memset(T.h[:, H0 + 2047:H0 + 2048], 0.0))
+    def by_source(qs):
+        need("V", t_ls)
+        for q in qs:
+            need("Y", v(V.tensor_copy(out=T.lc[:, BY * q:BY * q + BY], in_=T.ls[0:16, q:192:4])))
+            for k in range(2):
+                t_of = dma("d_of", Y.dma_start(out=T.of[16 * k + 4 * q:16 * k + 4 * q + 4, 0:NAT], in_=T.lc[:, BY * q:BY * q + BY]))
+        return t_of
 
-    def listed(q, j, t):
-        d = order[j]
-        return move(q, T.xs[:, 4 * C1 * j + t:4 * C1 * (j + 1):4], T.xb[:, 0:2048].indirect(T.so[:, 80 * t + 20 * d:80 * t + 20 * d + 20]), t_x, t_so)
+    PC = dict(CFG["pieces"], **{str(j): (j, 0, C1) for j in range(3)})
+    ENG = {"f": far_eng, "n": near_eng, "e": far_eng[0::2], "o": far_eng[1::2], "l": far_eng[:4], "h": far_eng[4:], "m": near_eng[0::2], "k": near_eng[1::2]}
+    lands = [0, 0, 0, 0]
+    DV = CFG["deliv"]
+    HS, PLX = CFG["pl"]
+
+    def listed(q, name, t):
+        j, c0, c1 = PC[name]
+        o = 80 * t + 20 * order[j]
+        return move(q, T.xs[:, 4 * (C1 * j + c0) + t:4 * (C1 * j + c1):4], T.xb[:, 0:2048].indirect(T.so[:, o + c0 // 16:o + c1 // 16]), t_x, t_so[t])
 
     def send(parts):
         ts = []
@@ -137,40 +177,86 @@ def rank_program(g, core, T, topo):
             count["sent"] = count.get("sent", 0) + len(es)
         g.remote_dma_fused(ts, local_sem=T.sem.sent)
 
-    def part1(kind, j):
-        d = order[j]
-        k = slot(r, d)
-        if kind == "codes":
-            o, i = T.c1[:, C1 * k:C1 * k + C1].bitcast(U8), T.xsq[:, C1 * j:C1 * j + C1].bitcast(U8)
+    def part1(kind, name, eng):
+        if kind == "c":
+            j, c0, c1 = PC[name]
+            k = [k for k, a in enumerate(DV) if a[0] == j and a[1] <= c0 and c1 <= a[2]][0]
+            o, i = T.c1[:, C1 * j + c0:C1 * j + c1].bitcast(U8), T.xsq[:, C1 * j + c0:C1 * j + c1].bitcast(U8)
         else:
-            o, i = T.p1[:, C1 * k:C1 * k + C1], T.pl[:, PLX[j]:PLX[j] + C1]
-        return (o, i, d, "a1_%d" % k, near_eng if d in near else far_eng)
+            k = "abcd".index(name)
+            j, c0, c1, w = DV[k]
+            o, i = T.p1[:, NODES * (k + 1) - w:NODES * (k + 1)], T.pl[:, PLX[j] + c1 - w:PLX[j] + c1]
+        need("g", *[t for n, t in t_q.items() if PC[n][0] == j and PC[n][1] < c1 and c0 < PC[n][2]])
+        lands[k] += len(ENG[eng])
+        return (o, i, order[j], "a1_%d" % k, ENG[eng])
 
-    t_q = []
-    for j, share in enumerate(("VVSS", "VVSS", "VSSS")):
-        toks = [listed(q, j, t) for t, q in enumerate(share)]
-        need("V", *toks)
-        t_q.append(v(V.quantize_mx(out=T.xsq[:, C1 * j:C1 * j + C1], scales=T.pl[:, PLX[j]:PLX[j] + C1], in_=T.xs[:, 4 * C1 * j:4 * C1 * j + 4 * C1])))
-    need("g", t_q[0])
-    send([part1("codes", 0)])
-    send([part1("planes", 0)])
-    need("g", t_q[2])
-    send([part1("codes", 1), part1("codes", 2)])
-    send([part1("planes", 1), part1("planes", 2)])
+    def small_lists():
+        need("V", t_s2, t_ls)
+        if " H" in CFG["work"]:
+            v(V.tensor_copy(out=T.of[0:32, NAT:SN], in_=T.ls[:, 64:192]))
+            for i in range(3):
+                tok = v(V.tensor_scalar(out=T.of[0:32, SN + 12 * i:SN + 12 * i + 12], in0=T.ls[:, 192:204], scalar1=4.0, scalar2=float(i), op0=MULT, op1=ADD))
+            return tok
+        v(V.tensor_copy(out=T.of[0:32, NAT:SN4], in_=T.ls[:, 64:204]))
+        return v(V.tensor_scalar(out=T.of[0:32, SN4:SN4 + 12], in0=T.ls[:, 192:204], scalar1=4.0, scalar2=3.0, op0=MULT, op1=ADD))
 
-    need("V", t_w1)
-    t_xq = v(V.quantize_mx(out=T.xq[:, :], scales=T.xp[:, :], in_=T.xb[:, :]))
-    t_wq = [v(V.quantize_mx(out=T.w1q[:, 256 * k:256 * k + 256], scales=T.w1p[:, 256 * k:256 * k + 256], in_=T.w1b[:, 1024 * k:1024 * k + 1024])) for k in range(2)]
-    need("V", t_s2)
-    v(V.tensor_copy(out=T.of[0:32, SN:SN4], in_=T.s2[:, :]))
-    t_a = v(V.tensor_scalar(out=T.s3[:, :], in0=T.s2[:, :], scalar1=4.0, scalar2=3.0, op0=MULT, op1=ADD))
-    need("V", t_w2)
-    t_w2q = v(V.quantize_mx(out=T.w2q[:, :], scales=T.w2p[:, :], in_=T.w2b[:, :]))
-    need("V", t_a)
-    t_a = v(V.tensor_copy(out=T.of[0:32, SN4:OFW], in_=T.s3[:, :]))
-    need("V", t_a, t_of)
+    st = {}
+
+    def compose(w):
+        if w == "k1":
+            need("V", t_s4, t_ko)
+            st["k"] = v(V.tensor_scalar(out=T.k1[:, :], in0=T.s4[:, :], scalar1=2, scalar2=None, op0=AluOpType.arith_shift_right))
+        elif w == "k2":
+            need("V", st["k"])
+            st["k"] = v(V.tensor_scalar(out=T.k2[:, :], in0=T.k1[:, :], scalar1=-511 / 128, scalar2=None, op0=MULT))
+        elif w == "k3":
+            need("V", st["k"])
+            st["k"] = v(V.tensor_tensor(out=T.k3[:, :], in0=T.s4[:, :], in1=T.k2[:, :], op=ADD))
+        elif w == "k4":
+            need("V", st["k"])
+            st["k"] = v(V.tensor_scalar(out=T.ko[0:32, :], in0=T.k3[:, :], scalar1=128.0, scalar2=None, op0=MULT))
+        elif w == "k5":
+            st["k"] = move("V", T.ga[:, :], T.bye[:, 0:512].indirect(T.ko[:, :]), st["k"], t_bye)
+        elif w == "k6":
+            need("V", st["k"])
+            st["k"] = v(V.transpose(out=T.gt[:, :], in_=T.ga[0:32, :]))
+        elif w == "k7":
+            need("V", st["k"])
+            for e in range(4):
+                tok = v(V.tensor_copy(out=T.oc[:, 12 * e:12 * e + 12], in_=T.gt[0:16, e:192:16]))
+            need("Y", tok)
+            for k in range(8):
+                st["oc"] = dma("d_oc", Y.dma_start(out=T.of[16 * k:16 * k + 16, OC:OC + 48], in_=T.oc[:, :]))
+
+    t_q, t_wq, toks = {}, {}, {}
+    for w in CFG["front"].split():
+        if w == "L": t_sl = small_lists()
+        elif w[0] == "k": compose(w)
+        elif w[0] == "K": t_of = by_source([int(c) for c in w[1:] or "0123"])
+        elif w == "U":
+            need("V", t_w2)
+            t_w2q = v(V.quantize_mx(out=T.w2q[:, :], scales=T.w2p[:, :], in_=T.w2b[:, :]))
+        elif w == "X":
+            need("V", t_x)
+            t_xq = v(V.quantize_mx(out=T.xq[:, :], scales=T.xp[:, :], in_=T.xb[:, :]))
+        elif w[0] == "W":
+            k = int(w[1])
+            need("V", t_w1)
+            t_wq[k] = v(V.quantize_mx(out=T.w1q[:, 256 * k:256 * k + 256], scales=T.w1p[:, 256 * k:256 * k + 256], in_=T.w1b[:, 1024 * k:1024 * k + 1024]))
+        elif w[0] == "q":
+            j, c0, c1 = PC[w[1]]
+            need("V", *toks[w[1]])
+            t_q[w[1]] = v(V.quantize_mx(out=T.xsq[:, C1 * j + c0:C1 * j + c1], scales=T.pl[:, PLX[j] + c0:PLX[j] + c1], in_=T.xs[:, 4 * (C1 * j + c0):4 * (C1 * j + c1)]))
+        else:
+            toks[w[0]] = [listed(q, w[0], t) for t, q in enumerate(w[1:])]
+    for call in CFG["calls"].split():
+        send([part1(*w) for w in call.split("+")])
+    q = "Y" if CFG["repdma"] else "V"
+    need(q, t_sl, t_of)
     for k in (1, 2, 3):
-        t_off = v(V.tensor_copy(out=T.of[32 * k:32 * k + 32, :], in_=T.of[0:32, :]))
+        w = SN + (36 if " H" in CFG["work"] else 24)
+        o, i = T.of[32 * k:32 * k + 32, 0:w], T.of[0:32, 0:w]
+        t_off = dma("d_off", Y.dma_start(out=o, in_=i)) if CFG["repdma"] else v(V.tensor_copy(out=o, in_=i))
 
     free = {}
     full = {}
@@ -190,61 +276,59 @@ def rank_program(g, core, T, topo):
         full.setdefault(i, []).append(free[bank])
 
     need("P", t_xq)
-    toks = [product(i, i, T.xq[:, :], T.xp[:, :], NODES) for i in range(4)]
-    for i, q in enumerate("SSSV"):
-        evacuate(q, i, i, 0, NODES, toks[i])
-    for a, sd in enumerate(arrive):
-        k = slot(sd, r)
-        es = near_eng if sd in near else far_eng
-        need("P", ("a1_%d" % k, 2 * len(es)))
-        b0 = 0 if a == 1 else 4
-        toks = [product(i, b0 + i, T.c1[:, C1 * k:C1 * k + C1], T.p1[:, C1 * k:C1 * k + C1], C1) for i in range(4)]
-        for i, q in enumerate("SVVV" if a == 2 else "SVSV"):
-            evacuate(q, i, b0 + i, NODES + C1 * sd, C1, toks[i])
+    mm = CFG["mm"].split()
+    made = {}
+
+    def bring(q, name):
+        while name not in made:
+            n = len(made)
+            i = int(mm[n][1])
+            assert n < 8 or mm[n - 8] in brought
+            if mm[n][0] == "o":
+                made[mm[n]] = (n % 8, 0, NODES, product(i, n % 8, T.xq[:, :], T.xp[:, :], NODES))
+            else:
+                k = "abcd".index(mm[n][0])
+                j, c0, c1, w = DV[k]
+                need("P", ("a1_%d" % k, lands[k]))
+                made[mm[n]] = (n % 8, NODES + C1 * order[j] + c0, c1 - c0,
+                               product(i, n % 8, T.c1[:, C1 * j + c0:C1 * j + c1], T.p1[:, NODES * (k + 1) - (c1 - c0):NODES * (k + 1)], c1 - c0))
+        evacuate(q, int(name[1]), *made[name])
+        brought.append(name)
+    brought = []
 
     M = [T["m%d" % i] for i in range(4)]
     A = {2: T.a2, 3: T.a3}
     last = {}
+    piece = {"": (0, 512), "a": (0, 256), "b": (256, 512), "c": (256, 384), "d": (384, 512), "e": (0, 128), "f": (128, 256), "h": (0, 384), "i": (128, 512)}
 
-    def src(i, e, n0, n1): return R[i][:, 0:W1T].indirect(T.of[:, BY * e + n0 // 16:BY * e + n1 // 16])
+    def src(i, c0, c1): return R[i][:, 0:W1T].indirect(T.of[:, c0:c1])
+    def res(i, n0, n1): return M[i][:, n0:n1] if i < 2 else M[i][:, 4 * n0 + 3:4 * n1:4]
+    def on(i, n0, n1): return [t for (a, b, c), t in last.items() if a == i and b < n1 and n0 < c]
 
-    def first(i, n0, n1):
-        last[i, n0] = move("S", M[i][:, n0:n1], src(i, 0, n0, n1), t_off, t_r, *full[i])
+    def first(q, i, n0, n1):
+        last[i, n0, n1] = move(q, res(i, n0, n1), src(i, 16 + n0 // 16, 16 + n1 // 16), t_off, t_r, t_m2, *full[i])
 
-    def more(i, e, n0, n1):
-        need("V", last[i, n0], *full[i])
-        last[i, n0] = v(V.tensor_tensor(out=M[i][:, n0:n1], in0=src(i, e, n0, n1), in1=M[i][:, n0:n1], op=MAX))
+    def more(i, e, n0, n1, out=None):
+        need("V", t_off, *on(i, n0, n1), *full[i])
+        last[i, n0, n1] = v(V.tensor_tensor(out=res(i, n0, n1) if out is None else out, in0=src(i, BY * e + 16 + n0 // 16, BY * e + 16 + n1 // 16), in1=res(i, n0, n1), op=MAX))
+        return last[i, n0, n1]
 
     def four(i, n0, n1):
-        last[i, n0] = move("S", A[i][:, 4 * n0:4 * n1], R[i][:, 0:W1T].indirect(T.of[:, NAT + n0 // 4:NAT + n1 // 4]), t_off, t_r, *full[i])
+        last[i, n0, n1] = move("S", A[i][:, 4 * n0:4 * n1], src(i, NAT + n0 // 4, NAT + n1 // 4), t_off, t_r, *full[i])
 
-    def scan(i, n0, n1):
-        need("V", last[i, n0], t_mask)
-        last[i, n0] = v(V.tensor_tensor_scan(M[i][:, 4 * n0:4 * n1], T.mask[:, 0:4 * (n1 - n0)], A[i][:, 4 * n0:4 * n1], 0.0, MULT, MAX))
+    scans = []
 
-    def table(i): return [t for (a, _), t in last.items() if a == i]
+    def scan(i, n0, n1, out=None):
+        need("V", *on(i, n0, n1), t_mask)
+        last[i, n0, n1] = v(V.tensor_tensor_scan(M[i][:, 4 * n0:4 * n1] if out is None else out, T.mask[:, 0:4 * (n1 - n0)], A[i][:, 4 * n0:4 * n1], 0.0, MULT, MAX))
+        scans.append(last[i, n0, n1])
+        return last[i, n0, n1]
 
-    def slots(q, i):
-        win, c = (M[i][:, 0:512], SN) if i < 2 else (M[i][:, 0:2048], SN4)
-        return move(q, T.hs[:, i:768:4], win.indirect(T.of[:, c:c + 12]), *table(i))
+    def slots(q, i, c0, c1):
+        c = SN if i < 2 else SN4
+        return move(q, T.hs[:, 64 * c0 + i:64 * c1:4], M[i][:, :].indirect(T.of[:, c + c0:c + c1]), *on(i, 0, NODES))
 
-    first(0, 0, 256); first(0, 256, 512); first(1, 0, 512)
-    four(2, 0, 256); four(2, 256, 512); four(3, 0, 256); four(3, 256, 384); four(3, 384, 512)
-    need("V", t_off)
-    more(0, 1, 0, 256); more(0, 1, 256, 512); more(0, 2, 0, 256)
-    more(1, 1, 0, 512); more(0, 2, 256, 512); more(0, 3, 0, 256)
-    scan(2, 0, 256); more(0, 3, 256, 512); more(1, 2, 0, 512)
-    scan(2, 256, 512); more(1, 3, 0, 512)
-    t_hs = [slots("V", 0)]
-    scan(3, 0, 256)
-    t_hs.append(slots("V", 1))
-    scan(3, 256, 384); scan(3, 384, 512)
-    t_hs.append(slots("S", 2))
-    t_hs.append(slots("V", 3))
-    need("V", *t_hs)
-    t_hq = v(V.quantize_mx(out=T.hsq[:, :], scales=T.pl[:, HS:HS + 3 * C2], in_=T.hs[:, :]))
 
-    need("g", t_hq)
     parts = []
     quarter, half = len(far_eng) // 4, len(near_eng) // 2
     engs = {far[0]: (far_eng[:quarter], far_eng[quarter:2 * quarter]), far[1]: (far_eng[2 * quarter:3 * quarter], far_eng[3 * quarter:]),
@@ -257,23 +341,80 @@ def rank_program(g, core, T, topo):
         w0 = HS + c0 - (PW - C2 if a == 0 else 0)
         parts.append((codes.bitcast(U8), T.hsq[:, c0:c0 + C2].bitcast(U8), d, "a2", engs[d][0]))
         parts.append((plane, T.pl[:, w0:w0 + PW], d, "a2", engs[d][1]))
-    send(parts)
+
+    def send2(tok):
+        need("g", tok)
+        send(parts)
     t_a2 = ("a2", len(far_eng) + len(near_eng))
 
     def product2(bank, rhs, plane, n):
-        need("P", free[bank])
+        need("P", free[bank], st["w2q"])
         return p(P.matmul_mx(T.ps[:, 512 * bank:512 * bank + n], T.w2q[:, :], T.w2p[:, :], rhs, plane, True, True))
-    need("P", t_w2q)
-    toks = []
-    for i, q in enumerate("VVVS"):
-        toks.append(move(q, T.h[:, i:2048:4], M[i][:, :] if i < 2 else M[i][:, 3:2048:4], *table(i)))
-    need("V", *toks)
-    t_own = []
-    for k, q in enumerate("SV"):
-        t_h = v(V.quantize_mx(out=T.hq[:, 256 * k:256 * k + 256], scales=T.hp[:, 256 * k:256 * k + 256], in_=T.h[:, 1024 * k:1024 * k + 1024]))
-        need("P", t_h)
-        t_own.append(product2(k, T.hq[:, 256 * k:256 * k + 256], T.hp[:, 256 * k:256 * k + 256], 256))
-    t_tab = [move(q, T.u[:, 256 * k:256 * k + 256], T.ps[:, 512 * k:512 * k + 256], t_own[k]) for k, q in enumerate("SV")]
+    def via(i, e): return src(i, OC + 12 * e, OC + 12 * e + 12)
+    def inh(n0, n1): return [t for (b, c, t) in into if b < n1 and n0 < c]
+
+    t_hs, into, t_own, t_tab = [], [], {}, []
+    for w in CFG["work"].split():
+        if w[0] in "oabcd": bring(w[2], w[:2])
+        elif w[0] == "f": first("S", int(w[1]), *piece[w[2:]])
+        elif w[0] == "F": first("V", int(w[1]), *piece[w[2:]])
+        elif w[0] == "g": four(int(w[1]), *piece[w[2:]])
+        elif w[0] == "m": more(int(w[1]), int(w[2]), *piece[w[3:]])
+        elif w[0] == "s": scan(int(w[1]), *piece[w[2:]])
+        elif w[0] == "z":
+            n0, n1 = piece[w[2:]]
+            i = int(w[1])
+            into.append((n0, n1, scan(i, n0, n1, T.h[:, H0 + i - 3 + 4 * n0:H0 + i - 3 + 4 * n1])))
+        elif w[0] == "H":
+            i, (c0, c1) = int(w[2]), {"": (0, 12), "a": (0, 6), "b": (6, 12)}[w[3:]]
+            t_hs.append(move(w[1], T.hs[:, 64 * c0 + i:64 * c1:4], T.h[:, H0:H0 + 2048].indirect(T.of[:, SN + 12 * i + c0:SN + 12 * i + c1]),
+                             t_h0, *inh(0, NODES), *[st[z] for z in "Z" if z in st and (w[1] == "S" or CFG["waw"])]))
+            st["H"] = list(t_hs)
+        elif w[0] == "M":
+            i, (n0, n1) = int(w[1]), piece[w[3:]]
+            need("V", *[t for t in inh(n0, n1 + (i == 3)) if t in scans], *st.get("H", []))
+            into.append((n0, n1, more(i, int(w[2]), n0, n1, T.h[:, H0 + 4 * n0 + i:H0 + 4 * n1:4])))
+        elif w[0] == "i":
+            i, (n0, n1) = int(w[2]), piece[w[3:]]
+            clob = [t for t in inh(n0, n1 + (i == 3)) if t in scans]
+            into.append((n0, n1, move(w[1], T.h[:, H0 + 4 * n0 + i:H0 + 4 * n1:4], res(i, n0, n1), *on(i, n0, n1), *clob, *st.get("H", []))))
+        elif w[0] == "h":
+            n0, n1 = piece[w[1:]]
+            need("V", *inh(n0, n1))
+            t_h = v(V.quantize_mx(out=T.hq[:, n0:n1], scales=T.hp[:, n0:n1], in_=T.h[:, H0 + 4 * n0:H0 + 4 * n1]))
+            need("P", t_h)
+            bank = 4 + len(t_own)
+            t_own[w[1:]] = (bank, product2(bank, T.hq[:, n0:n1], T.hp[:, n0:n1], n1 - n0))
+        elif w[0] == "u":
+            (n0, n1), (bank, tok) = piece[w[2:]], t_own[w[2:]]
+            t_tab.append(move(w[1], T.u[:, n0:n1], T.ps[:, 512 * bank:512 * bank + n1 - n0], tok))
+        elif w == "T": t_u = v(V.memset(T.u[:, NODES + C2 * r:NODES + C2 * r + C2], 0.0))
+        elif w == "U":
+            if "T" not in CFG["work"]: t_u = v(V.memset(T.u[:, NODES + C2 * r:NODES + C2 * r + C2], 0.0))
+            need("V", t_w2)
+            st["w2q"] = v(V.quantize_mx(out=T.w2q[:, :], scales=T.w2p[:, :], in_=T.w2b[:, :]))
+        elif w == "Q":
+            need("V", *t_hs)
+            send2(v(V.quantize_mx(out=T.hsq[:, :], scales=T.pl[:, HS:HS + 3 * C2], in_=T.hs[:, :])))
+        elif w[0] == "k": compose(w)
+        elif w[0] == "n":
+            i, e = int(w[1]), int(w[2])
+            if e == 0:
+                st["n", i] = move("S", T.b1[:, i - 2, :], via(i, 0), st["oc"], t_r, *full[i])
+            else:
+                need("V", st["n", i], st["oc"], *full[i])
+                st["n", i] = v(V.tensor_tensor(out=T.hs[:, i:768:4] if e == 3 else T.b1[:, i - 2, :], in0=via(i, e), in1=T.b1[:, i - 2, :], op=MAX))
+                if e == 3: t_hs.append(st["n", i])
+        elif w == "N":
+            for e in range(4):
+                st["N"] = move("S", T.b4[:, e:768:4], via(3, e), st["oc"], t_r, *full[3])
+        elif w == "Z":
+            need("V", st["N"], t_mask)
+            st["Z"] = v(V.tensor_tensor_scan(T.hs[:, :], T.mask[:, 0:768], T.b4[:, :], 0.0, MULT, MAX))
+            t_hs.append(st["Z"])
+        else:
+            need(w[0], *[st[z] for z in "Z" if z in st])
+            t_hs.append(slots(w[0], int(w[1]), *{"": (0, 12), "a": (0, 6), "b": (6, 12)}[w[2:]]))
     need("P", t_a2)
     ta = product2(2, T.c2[:, :], T.p2[:, PW - C2:PW + C2], 2 * C2)
     tb = product2(3, T.hq[:, NODES - C2:NODES + C2], T.hp[:, NODES - C2:NODES + C2], 2 * C2)
@@ -282,15 +423,17 @@ def rank_program(g, core, T, topo):
     t_tab.append(move("V", T.u[:, NODES + C2 * a:NODES + C2 * (a + 2)], T.ps[:, 1024:1024 + 2 * C2], ta))
     t_tab.append(move("S", T.u[:, NODES + C2 * b:NODES + C2 * (b + 1)], T.ps[:, 1536 + C2:1536 + 2 * C2], tb))
 
-    def tgt(e, c0=0, c1=16): return T.u[:, 0:W2T].indirect(T.of[:, BY * e + 32 + c0:BY * e + 32 + c1])
-    tok = move("V", T.yb[:, 0:128], tgt(0, 0, 8), t_u, *t_tab)
-    t_s = move("S", T.yb[:, 128:256], tgt(0, 8, 16), t_u, *t_tab)
-    need("V", t_s)
-    for e in (1, 2, 3):
-        need("V", tok)
-        tok = v(V.tensor_tensor(out=T.yb[:, :], in0=tgt(e), in1=T.yb[:, :], op=MAX))
-    need("Y", tok)
-    t_y = dma("d_y", Y.dma_start(out=T.y[:, :], in_=T.yb[:, :]))
+    def tgt(e, c0=0, c1=16): return T.u[:, 0:W2T].indirect(T.of[:, BY * e + c0:BY * e + c1])
+    cuts = CFG["ycuts"]
+    tok = [move(q, T.yb[:, 16 * c0:16 * c1], tgt(0, c0, c1), t_u, *t_tab) for q, c0, c1 in cuts]
+    for w in CFG["yorder"].split():
+        k, e = int(w[0]), int(w[1])
+        _, c0, c1 = cuts[k]
+        need("V", tok[k])
+        tok[k] = v(V.tensor_tensor(out=T.yb[:, 16 * c0:16 * c1], in0=tgt(e, c0, c1), in1=T.yb[:, 16 * c0:16 * c1], op=MAX))
+    for q, c0, c1 in CFG["ystore"]:
+        need(q, *[t for t, (_, a, b) in zip(tok, cuts) if a < c1 and c0 < b])
+        t_y = dma("d_y", queues[q].dma_start(out=T.y[:, 16 * c0:16 * c1], in_=T.yb[:, 16 * c0:16 * c1]))
 
     need("g", ("sent", count["sent"]))
     need("Y", t_y, *[(k, count[k]) for k in ("cv", "cs", "ct")])

@@ -1,4 +1,3 @@
-import numpy as np
 from concourse.bass import DstId, RemoteDMATransfer
 from concourse.mybir import dt, AluOpType, ActivationFunctionType
 
@@ -6,9 +5,14 @@ N, NODES, TG, C1, C2 = 4, 512, 256, 320, 64
 W1T = NODES + N * C1
 W2T = NODES + N * C2
 F8 = "float8_e4m3fn_x4"
-PW = 4 * C2
-BY, NAT, SN, SN4, OC, OFW = 48, 192, 320, 332, 360, 408
+FAR0, FAR1, NEAR = 0, 1, 2
+BASE = {FAR0: 0, NEAR: C1, FAR1: 2 * C1}
+PIECES = {"A": (FAR0, 0, 128), "B": (FAR0, 128, C1), "C": (NEAR, 0, 192), "D": (NEAR, 192, C1), "E": (FAR1, 0, C1)}
+LOTS = {"a": (FAR0, 0, C1, C1), "b": (NEAR, 0, 192, C1), "c": (FAR1, 0, C1, C1), "d": (NEAR, 192, C1, 512)}
+PRODUCTS = [(lot, i) for lot in "oab" for i in range(4)] + [("c", 0), ("c", 1), ("d", 0), ("d", 1)] + [(lot, i) for i in (2, 3) for lot in "cd"]
+BY, NAT, SN, OC, OFW = 48, 192, 320, 360, 408
 H0 = 16
+HS = 3 * C1
 SCRATCH = {
     "xb": ("sbuf", [128, 2048], "bfloat16"), "xq": ("sbuf", [128, 512], F8), "xp": ("sbuf", [128, 512], "uint8"),
     "w1b": ("sbuf", [128, 2048], "bfloat16"), "w1q": ("sbuf", [128, 512], F8), "w1p": ("sbuf", [128, 512], "uint8"),
@@ -16,36 +20,24 @@ SCRATCH = {
     "xs": ("sbuf", [128, 12 * C1], "bfloat16"), "xsq": ("sbuf", [128, 3 * C1], F8),
     "hs": ("sbuf", [128, 12 * C2], "bfloat16"), "hsq": ("sbuf", [128, 3 * C2], F8),
     "pl": ("sbuf", [128, 3 * C1 + 3 * C2], "uint8"),
-    "c1": ("sbuf", [128, 3 * C1], F8), "p1": ("sbuf", [128, 4 * NODES], "uint8"),
-    "c2": ("sbuf", [128, 2 * C2], F8), "p2": ("sbuf", [128, 2 * PW], "uint8"),
+    "c1": ("sbuf", [128, 3 * C1], F8), "p1": ("sbuf", [128, 4 * 512], "uint8"),
+    "c2": ("sbuf", [128, 3 * C2], F8), "p2": ("sbuf", [128, 3 * C2], "uint8"),
     "r0": ("sbuf", [128, W1T], "bfloat16"), "r1": ("sbuf", [128, W1T], "bfloat16"),
     "r2": ("sbuf", [128, W1T], "bfloat16"), "r3": ("sbuf", [128, W1T], "bfloat16"),
-    "m0": ("sbuf", [128, 512], "bfloat16"), "m1": ("sbuf", [128, 512], "bfloat16"),
-    "a2": ("sbuf", [128, 2048], "bfloat16"), "a3": ("sbuf", [128, 2048], "bfloat16"),
-    "m2": ("sbuf", [128, 2048], "bfloat16"), "m3": ("sbuf", [128, 2048], "bfloat16"),
-    "mask": ("sbuf", [128, 1024], "bfloat16"),
-    "h": ("sbuf", [128, 2064], "bfloat16"), "hq": ("sbuf", [128, NODES + C2], F8), "hp": ("sbuf", [128, NODES + PW], "uint8"),
+    "m0": ("sbuf", [128, 512], "bfloat16"), "m1": ("sbuf", [128, 512], "bfloat16"), "m3": ("sbuf", [128, 512], "bfloat16"),
+    "a2": ("sbuf", [128, 2048], "bfloat16"), "a3": ("sbuf", [128, 1024], "bfloat16"), "s3": ("sbuf", [128, 1024], "bfloat16"),
+    "b3": ("sbuf", [128, 768], "bfloat16"), "t3": ("sbuf", [128, 768], "bfloat16"), "mask": ("sbuf", [128, 1024], "bfloat16"),
+    "h": ("sbuf", [128, H0 + 2048], "bfloat16"), "hq": ("sbuf", [128, 512], F8), "hp": ("sbuf", [128, 512], "uint8"),
     "u": ("sbuf", [128, W2T], "float32"), "yb": ("sbuf", [128, TG], "float32"),
     "sl": ("sbuf", [128, 80], "int32"), "so": ("sbuf", [128, 320], "uint16"),
-    "ls": ("sbuf", [32, 204], "int32"), "lc": ("sbuf", [16, 192], "uint16"),
-    "of": ("sbuf", [128, OFW], "uint16"),
+    "ls": ("sbuf", [32, 204], "int32"), "lc": ("sbuf", [16, 192], "uint16"), "of": ("sbuf", [128, OFW], "uint16"),
     "s4": ("sbuf", [32, 12], "int32"), "k1": ("sbuf", [32, 12], "int32"), "k2": ("sbuf", [32, 12], "float32"),
     "k3": ("sbuf", [32, 12], "float32"), "ko": ("sbuf", [128, 12], "uint16"), "bye": ("sbuf", [128, 512], "int32"),
     "ga": ("sbuf", [128, 192], "float32"), "gt": ("sbuf", [32, 192], "float32"), "oc": ("sbuf", [16, 48], "uint16"),
-    "b1": ("sbuf", [128, 2, 192], "bfloat16"), "b4": ("sbuf", [128, 768], "bfloat16"),
     "ps": ("psum", [128, 4096], "float32"),
 }
-SEMAPHORES = ["cg", "cv", "cs", "ct", "d_snd", "d_ls", "d_x", "d_s2", "d_w1", "d_w2", "d_of", "d_off", "d_bye", "d_s4", "d_oc", "d_y",
-              "a1_0", "a1_1", "a1_2", "a1_3", "a2", "sent"]
-CFG = dict(
-    pieces={"A": (0, 0, 128), "B": (0, 128, 320), "C": (2, 0, 192), "D": (2, 192, 320)},
-    deliv=[(0, 0, 320, 320), (2, 0, 192, 320), (1, 0, 320, 320), (2, 192, 320, 512)], pl=(640, [0, 832, 320]),
-    front="AVVSS K0 qA BVVSS K1 qB CVSSS K23 qC X 1VSSS W0 k1 q1 DVSSS k2 W1 qD L", calls="cAf cBf+cCn paf+pbn c1f pcf cDm+pdk", repdma=True,
-    mm="o0 o1 o2 o3 a0 a1 a2 a3 b0 b1 b2 b3 c0 c1 d0 d1 c2 d2 c3 d3",
-    work="k3 o0S o1V k4 o2S o3V k5 a0S a1V k6 a2S a3V k7 b0S b1S b2S b3S c0V d0V c1V d1V "
-         "f0 c2V d2V f1 g2a g2b c3S d3V N g3e m01 m11 m02 m12 z2a z2b M03a M13 M03b Z U T HV0 HS1 HV2 "
-         "g3f g3c g3d Q s3e s3f s3c iV3a s3d ha iS3c hc iV3d hd uVa uSc uVd",
-    inter="SSVV", ycuts=[("V", 0, 6), ("S", 6, 16)], yorder="01 11 02 12 03 13", ystore=[("Y", 0, 6), ("S", 6, 16)], xfirst=True, sndn=2, waw=True)
+SEMAPHORES = ["cg", "cv", "cs", "ct", "d_snd", "d_ls", "d_x", "d_s2", "d_w0", "d_w1", "d_w2", "d_of", "d_off", "d_bye", "d_s4",
+              "d_oc", "d_y", "a1_a", "a1_b", "a1_c", "a1_d", "a2", "sent"]
 
 
 def rank_program(g, core, T, topo):
@@ -66,374 +58,321 @@ def rank_program(g, core, T, topo):
         return (sem, count[sem])
 
     def need(q, *toks):
+        most = {}
         for sem, k in toks:
+            most[sem] = max(k, most.get(sem, 0))
+        for sem, k in most.items():
             if seen.get((q, sem), 0) < k:
                 queues[q].wait_ge(T.sem[sem], k)
                 seen[(q, sem)] = k
 
     def v(ins): return done("cv", ins)
-    def s(ins): return done("cs", ins)
-    def p(ins): return done("ct", ins)
     def dma(sem, ins): return done(sem, ins, 16)
 
     def move(q, o, i, *toks):
         need(q, *toks)
-        return v(V.tensor_copy(out=o, in_=i)) if q == "V" else s(S.activation(out=o, in_=i, func=COPY))
+        return v(V.tensor_copy(out=o, in_=i)) if q == "V" else done("cs", S.activation(out=o, in_=i, func=COPY))
+
+    def quantise(codes, plane, tile, *toks):
+        need("V", *toks)
+        return v(V.quantize_mx(out=codes, scales=plane, in_=tile))
+
+    def zeros(ap, n): return done("cg", g.iota(ap, [[0, n]], 0, 0, allow_small_or_imprecise_dtypes=True))
 
     others = [d for d in range(N) if d != r]
     me = T.cores[r]
     far = [d for d in others if topo.chip(T.cores[d]) != topo.chip(me)]
     far.sort(key=lambda d: topo.die(T.cores[d]) != topo.die(me))
-    near = [d for d in others if d not in far]
-    order = [far[0], far[1], near[0]]
-    far_eng = topo.engines(me, T.cores[far[0]])
-    near_eng = [e for e in topo.engines(me, T.cores[near[0]]) if e not in far_eng]
+    rank = far + [d for d in others if d not in far]
+    far_eng = topo.engines(me, T.cores[rank[FAR0]])
+    near_eng = [e for e in topo.engines(me, T.cores[rank[NEAR]]) if e not in far_eng]
 
-    def bits(es): return sum(1 << e for e in es)
     def slot(a, b): return a - (1 if a > b else 0)
     runs = []
     for d in others:
         if runs and runs[-1][0] + runs[-1][1] == d: runs[-1][1] += 1
         else: runs.append([d, 1])
 
-    def pair(d):
-        return min(a for a in range(N - 1) if d not in (a, a + 1))
-
-    SG = CFG["sndn"]
-    for k in range(SG):
-        t_snd = dma("d_snd", (Y, S)[k % 2].dma_start(out=T.sl[16 * k:16 * k + 16, :], in_=T.snd1[:, :]))
-    for w in ("xl" if CFG["xfirst"] else "lx"):
-        if w == "l":
-            dma("d_ls", Y.dma_start(out=T.ls[0:16, 64:192], in_=T.src1[:, :]))
-            t_ls = dma("d_ls", S.dma_start(out=T.ls[0:16, 0:64], in_=T.src2[:, :]))
-        else:
-            dma("d_x", S.dma_start(out=T.xb[64:128, :], in_=T.x[64:128, :]))
-            t_x = dma("d_x", Y.dma_start(out=T.xb[0:64, :], in_=T.x[0:64, :]))
-    dma("d_s2", S.dma_start(out=T.ls[16:32, 64:192], in_=T.src1[:, :]))
-    for k in range(2):
-        c = 192
-        for d, n in runs:
-            t_s2 = dma("d_s2", (Y, S)[k].dma_start(out=T.ls[16 * k:16 * k + 16, c:c + 4 * n], in_=T.snd2[:, 4 * d:4 * d + 4 * n]))
-            c += 4 * n
-    t_w1 = dma("d_w1", Y.dma_start(out=T.w1b[:, :], in_=T.w1[:, :]))
-    t_w2 = dma("d_w2", Y.dma_start(out=T.w2b[:, :], in_=T.w2[:, :]))
-
-    R = [T["r%d" % i] for i in range(4)]
-    if "k7" in CFG["work"]:
-        t_s4 = v(V.memset(T.s4[:, :], 0))
-        t_ko = v(V.memset(T.ko[:, :], 0))
-    t_one = v(V.memset(T.mask[:, :], 1.0))
-    for i in range(4):
-        t_r = v(V.memset(R[i][:, NODES + C1 * r:NODES + C1 * r + C1], 0.0))
-
-    if "k7" in CFG["work"]:
-        t_bye = done("cg", g.iota(T.bye[:, :], [[0, 512]], 0, 0))
-        need("Y", t_bye, t_s4, t_ko)
-        for k in range(2):
-            for a in range(4):
-                t_bye = dma("d_bye", Y.dma_start(out=T.bye[16 * k:16 * k + 4, 128 * a:128 * a + 128], in_=T.src1[4 * a:4 * a + 4, :]))
-            c = 0
-            for d, n in runs:
-                c0 = k if c == 0 else 0
-                t_s4 = dma("d_s4", Y.dma_start(out=T.s4[16 * k:16 * k + 16, c + c0 - k:c + 4 * n - k], in_=T.snd2[:, 4 * d + c0:4 * d + 4 * n]))
-                c += 4 * n
-    t_m2 = done("cg", g.iota(T.m2[:, 0:1024], [[0, 1024]], 0, 0, allow_small_or_imprecise_dtypes=True)) if "f2" in CFG["work"] else t_r
-
-    need("V", t_snd)
-    for k in range(16 * SG, 128, 16 * SG):
-        t_a = v(V.tensor_copy(out=T.sl[k:k + 16 * SG, :], in_=T.sl[0:16 * SG, :]))
-    need("V", t_one)
-    t_mask = v(V.memset(T.mask[:, 0::4], 0.0))
-    if SG < 8: need("V", t_a)
-    t_so = {}
-    for t in (2, 0, 3, 1):
-        t_so[t] = v(V.tensor_scalar(out=T.so[:, 80 * t:80 * t + 80], in0=T.sl[:, :], scalar1=4.0, scalar2=float(t), op0=MULT, op1=ADD))
-    if " H" in CFG["work"]:
-        t_h0 = v(V.memset(T.h[:, H0 + 2047:H0 + 2048], 0.0))
-    def by_source(qs):
-        need("V", t_ls)
-        for q in qs:
-            need("Y", v(V.tensor_copy(out=T.lc[:, BY * q:BY * q + BY], in_=T.ls[0:16, q:192:4])))
-            for k in range(2):
-                t_of = dma("d_of", Y.dma_start(out=T.of[16 * k + 4 * q:16 * k + 4 * q + 4, 0:NAT], in_=T.lc[:, BY * q:BY * q + BY]))
-        return t_of
-
-    PC = dict(CFG["pieces"], **{str(j): (j, 0, C1) for j in range(3)})
-    ENG = {"f": far_eng, "n": near_eng, "e": far_eng[0::2], "o": far_eng[1::2], "l": far_eng[:4], "h": far_eng[4:], "m": near_eng[0::2], "k": near_eng[1::2]}
-    lands = [0, 0, 0, 0]
-    DV = CFG["deliv"]
-    HS, PLX = CFG["pl"]
-
-    def listed(q, name, t):
-        j, c0, c1 = PC[name]
-        o = 80 * t + 20 * order[j]
-        return move(q, T.xs[:, 4 * (C1 * j + c0) + t:4 * (C1 * j + c1):4], T.xb[:, 0:2048].indirect(T.so[:, o + c0 // 16:o + c1 // 16]), t_x, t_so[t])
-
-    def send(parts):
+    def send(*parts):
         ts = []
         for o, i, d, sm, es in parts:
             rid, pid, _ = topo.addr(T.cores[d])
-            ts.append(RemoteDMATransfer(dst_ids=[DstId(rid=rid, pnc=pid)], dma_engine_mask=bits(es), remote_sem=T.sem[sm], src=i, dst=o))
+            ts.append(RemoteDMATransfer(dst_ids=[DstId(rid=rid, pnc=pid)], dma_engine_mask=sum(1 << e for e in es), remote_sem=T.sem[sm], src=i, dst=o))
             count["sent"] = count.get("sent", 0) + len(es)
         g.remote_dma_fused(ts, local_sem=T.sem.sent)
 
-    def part1(kind, name, eng):
-        if kind == "c":
-            j, c0, c1 = PC[name]
-            k = [k for k, a in enumerate(DV) if a[0] == j and a[1] <= c0 and c1 <= a[2]][0]
-            o, i = T.c1[:, C1 * j + c0:C1 * j + c1].bitcast(U8), T.xsq[:, C1 * j + c0:C1 * j + c1].bitcast(U8)
-        else:
-            k = "abcd".index(name)
-            j, c0, c1, w = DV[k]
-            o, i = T.p1[:, NODES * (k + 1) - w:NODES * (k + 1)], T.pl[:, PLX[j] + c1 - w:PLX[j] + c1]
-        need("g", *[t for n, t in t_q.items() if PC[n][0] == j and PC[n][1] < c1 and c0 < PC[n][2]])
-        lands[k] += len(ENG[eng])
-        return (o, i, order[j], "a1_%d" % k, ENG[eng])
+    dma("d_snd", Y.dma_start(out=T.sl[0:16, :], in_=T.snd1[:, :]))
+    t_snd = dma("d_snd", S.dma_start(out=T.sl[16:32, :], in_=T.snd1[:, :]))
+    dma("d_x", S.dma_start(out=T.xb[64:128, :], in_=T.x[64:128, :]))
+    t_x = dma("d_x", Y.dma_start(out=T.xb[0:64, :], in_=T.x[0:64, :]))
+    dma("d_ls", Y.dma_start(out=T.ls[0:16, 64:192], in_=T.src1[:, :]))
+    t_ls = dma("d_ls", S.dma_start(out=T.ls[0:16, 0:64], in_=T.src2[:, :]))
+    dma("d_s2", S.dma_start(out=T.ls[16:32, 64:192], in_=T.src1[:, :]))
+    for k, q in enumerate((Y, S)):
+        c = 192
+        for d, n in runs:
+            t_s2 = dma("d_s2", q.dma_start(out=T.ls[16 * k:16 * k + 16, c:c + 4 * n], in_=T.snd2[:, 4 * d:4 * d + 4 * n]))
+            c += 4 * n
+    t_w1 = [dma("d_w%d" % k, Y.dma_start(out=T.w1b[:, 1024 * k:1024 * k + 1024], in_=T.w1[:, 1024 * k:1024 * k + 1024])) for k in range(2)]
+    t_w2 = dma("d_w2", Y.dma_start(out=T.w2b[:, :], in_=T.w2[:, :]))
 
-    def small_lists():
-        need("V", t_s2, t_ls)
-        if " H" in CFG["work"]:
-            v(V.tensor_copy(out=T.of[0:32, NAT:SN], in_=T.ls[:, 64:192]))
-            for i in range(3):
-                tok = v(V.tensor_scalar(out=T.of[0:32, SN + 12 * i:SN + 12 * i + 12], in0=T.ls[:, 192:204], scalar1=4.0, scalar2=float(i), op0=MULT, op1=ADD))
-            return tok
-        v(V.tensor_copy(out=T.of[0:32, NAT:SN4], in_=T.ls[:, 64:204]))
-        return v(V.tensor_scalar(out=T.of[0:32, SN4:SN4 + 12], in0=T.ls[:, 192:204], scalar1=4.0, scalar2=3.0, op0=MULT, op1=ADD))
+    R = [T.r0, T.r1, T.r2, T.r3]
+    gap = [t[:, NODES + C1 * r:NODES + C1 * r + C1] for t in R]
+    t_s4 = v(V.memset(T.s4[:, :], 0))
+    t_ko = v(V.memset(T.ko[:, :], 0))
+    t_h0 = v(V.memset(T.h[:, H0 + 2047:H0 + 2048], 0.0))
+    t_one = v(V.memset(T.mask[:, :], 1.0))
+    full = {i: [v(V.memset(gap[i], 0.0))] for i in (0, 1)}
+    t_bye = done("cg", g.iota(T.bye[:, :], [[0, 512]], 0, 0))
+    t_u = zeros(T.u[:, NODES + C2 * r:NODES + C2 * r + C2], C2)
+    for i in (2, 3):
+        full[i] = [zeros(gap[i], C1)]
+    need("Y", t_bye, t_s4, t_ko)
+    for k in range(2):
+        for a in range(4):
+            t_bye = dma("d_bye", Y.dma_start(out=T.bye[16 * k:16 * k + 4, 128 * a:128 * a + 128], in_=T.src1[4 * a:4 * a + 4, :]))
+        c = 0
+        for d, n in runs:
+            c0 = k if c == 0 else 0
+            t_s4 = dma("d_s4", Y.dma_start(out=T.s4[16 * k:16 * k + 16, c + c0 - k:c + 4 * n - k], in_=T.snd2[:, 4 * d + c0:4 * d + 4 * n]))
+            c += 4 * n
 
-    st = {}
-
-    def compose(w):
-        if w == "k1":
-            need("V", t_s4, t_ko)
-            st["k"] = v(V.tensor_scalar(out=T.k1[:, :], in0=T.s4[:, :], scalar1=2, scalar2=None, op0=AluOpType.arith_shift_right))
-        elif w == "k2":
-            need("V", st["k"])
-            st["k"] = v(V.tensor_scalar(out=T.k2[:, :], in0=T.k1[:, :], scalar1=-511 / 128, scalar2=None, op0=MULT))
-        elif w == "k3":
-            need("V", st["k"])
-            st["k"] = v(V.tensor_tensor(out=T.k3[:, :], in0=T.s4[:, :], in1=T.k2[:, :], op=ADD))
-        elif w == "k4":
-            need("V", st["k"])
-            st["k"] = v(V.tensor_scalar(out=T.ko[0:32, :], in0=T.k3[:, :], scalar1=128.0, scalar2=None, op0=MULT))
-        elif w == "k5":
-            st["k"] = move("V", T.ga[:, :], T.bye[:, 0:512].indirect(T.ko[:, :]), st["k"], t_bye)
-        elif w == "k6":
-            need("V", st["k"])
-            st["k"] = v(V.transpose(out=T.gt[:, :], in_=T.ga[0:32, :]))
-        elif w == "k7":
-            need("V", st["k"])
-            for e in range(4):
-                tok = v(V.tensor_copy(out=T.oc[:, 12 * e:12 * e + 12], in_=T.gt[0:16, e:192:16]))
-            need("Y", tok)
-            for k in range(8):
-                st["oc"] = dma("d_oc", Y.dma_start(out=T.of[16 * k:16 * k + 16, OC:OC + 48], in_=T.oc[:, :]))
-
-    t_q, t_wq, toks = {}, {}, {}
-    for w in CFG["front"].split():
-        if w == "L": t_sl = small_lists()
-        elif w[0] == "k": compose(w)
-        elif w[0] == "K": t_of = by_source([int(c) for c in w[1:] or "0123"])
-        elif w == "U":
-            need("V", t_w2)
-            t_w2q = v(V.quantize_mx(out=T.w2q[:, :], scales=T.w2p[:, :], in_=T.w2b[:, :]))
-        elif w == "X":
-            need("V", t_x)
-            t_xq = v(V.quantize_mx(out=T.xq[:, :], scales=T.xp[:, :], in_=T.xb[:, :]))
-        elif w[0] == "W":
-            k = int(w[1])
-            need("V", t_w1)
-            t_wq[k] = v(V.quantize_mx(out=T.w1q[:, 256 * k:256 * k + 256], scales=T.w1p[:, 256 * k:256 * k + 256], in_=T.w1b[:, 1024 * k:1024 * k + 1024]))
-        elif w[0] == "q":
-            j, c0, c1 = PC[w[1]]
-            need("V", *toks[w[1]])
-            t_q[w[1]] = v(V.quantize_mx(out=T.xsq[:, C1 * j + c0:C1 * j + c1], scales=T.pl[:, PLX[j] + c0:PLX[j] + c1], in_=T.xs[:, 4 * (C1 * j + c0):4 * (C1 * j + c1)]))
-        else:
-            toks[w[0]] = [listed(q, w[0], t) for t, q in enumerate(w[1:])]
-    for call in CFG["calls"].split():
-        send([part1(*w) for w in call.split("+")])
-    q = "Y" if CFG["repdma"] else "V"
-    need(q, t_sl, t_of)
+    need("V", t_snd)
     for k in (1, 2, 3):
-        w = SN + (36 if " H" in CFG["work"] else 24)
-        o, i = T.of[32 * k:32 * k + 32, 0:w], T.of[0:32, 0:w]
-        t_off = dma("d_off", Y.dma_start(out=o, in_=i)) if CFG["repdma"] else v(V.tensor_copy(out=o, in_=i))
+        tok = v(V.tensor_copy(out=T.sl[32 * k:32 * k + 32, :], in_=T.sl[0:32, :]))
+    need("V", t_one)
+    t_mask = v(V.memset(T.mask[:, 0::4], 0.0))
+    need("V", tok)
+    t_so = {}
+    for t in (2, 0, 3, 1):
+        t_so[t] = v(V.tensor_scalar(out=T.so[:, 80 * t:80 * t + 80], in0=T.sl[:, :], scalar1=4.0, scalar2=float(t), op0=MULT, op1=ADD))
+
+    def by_source(*blocks):
+        need("V", t_ls)
+        for q in blocks:
+            need("Y", v(V.tensor_copy(out=T.lc[:, BY * q:BY * q + BY], in_=T.ls[0:16, q:192:4])))
+            for k in range(2):
+                tok = dma("d_of", Y.dma_start(out=T.of[16 * k + 4 * q:16 * k + 4 * q + 4, 0:NAT], in_=T.lc[:, BY * q:BY * q + BY]))
+        return tok
+
+    def composing():
+        need("V", t_s4, t_ko)
+        tok = v(V.tensor_scalar(out=T.k1[:, :], in0=T.s4[:, :], scalar1=2, scalar2=None, op0=AluOpType.arith_shift_right))
+        yield None
+        need("V", tok)
+        tok = v(V.tensor_scalar(out=T.k2[:, :], in0=T.k1[:, :], scalar1=-511 / 128, scalar2=None, op0=MULT))
+        yield None
+        need("V", tok)
+        tok = v(V.tensor_tensor(out=T.k3[:, :], in0=T.s4[:, :], in1=T.k2[:, :], op=ADD))
+        yield None
+        need("V", tok)
+        tok = v(V.tensor_scalar(out=T.ko[0:32, :], in0=T.k3[:, :], scalar1=128.0, scalar2=None, op0=MULT))
+        yield None
+        tok = move("V", T.ga[:, :], T.bye[:, 0:512].indirect(T.ko[:, :]), tok, t_bye)
+        yield None
+        need("V", tok)
+        tok = v(V.transpose(out=T.gt[:, :], in_=T.ga[0:32, :]))
+        yield None
+        need("V", tok)
+        for e in range(4):
+            tok = v(V.tensor_copy(out=T.oc[:, 12 * e:12 * e + 12], in_=T.gt[0:16, e:192:16]))
+        need("Y", tok)
+        for k in range(8):
+            tok = dma("d_oc", Y.dma_start(out=T.of[16 * k:16 * k + 16, OC:OC + 48], in_=T.oc[:, :]))
+        yield tok
+    compose = composing()
+
+    gathered, packed = {}, {}
+
+    def gather(name, engines):
+        j, c0, c1 = PIECES[name]
+        gathered[name] = []
+        for t, q in enumerate(engines):
+            o = 80 * t + 20 * rank[j]
+            gathered[name].append(move(q, T.xs[:, 4 * (BASE[j] + c0) + t:4 * (BASE[j] + c1):4],
+                                       T.xb[:, 0:2048].indirect(T.so[:, o + c0 // 16:o + c1 // 16]), t_x, t_so[t]))
+
+    def pack(name):
+        j, c0, c1 = PIECES[name]
+        c0, c1 = BASE[j] + c0, BASE[j] + c1
+        packed[name] = quantise(T.xsq[:, c0:c1], T.pl[:, c0:c1], T.xs[:, 4 * c0:4 * c1], *gathered[name])
+
+    def weights(k): return quantise(T.w1q[:, 256 * k:256 * k + 256], T.w1p[:, 256 * k:256 * k + 256], T.w1b[:, 1024 * k:1024 * k + 1024], t_w1[k])
+
+    gather("A", "VVSS"); by_source(0, 1); pack("A")
+    gather("B", "VVSS"); t_of = by_source(2, 3); pack("B")
+    gather("E", "VSSS")
+    t_xq = quantise(T.xq[:, :], T.xp[:, :], T.xb[:, :], t_x)
+    pack("E")
+    gather("C", "VSSS")
+    t_wq = [weights(0)]
+    next(compose)
+    pack("C")
+    next(compose)
+    gather("D", "SSSS")
+    t_wq.append(weights(1))
+    next(compose)
+    pack("D")
+    next(compose)
+    need("V", t_s2, t_ls)
+    v(V.tensor_copy(out=T.of[0:32, NAT:SN], in_=T.ls[:, 64:192]))
+    for i in range(3):
+        tok = v(V.tensor_scalar(out=T.of[0:32, SN + 12 * i:SN + 12 * i + 12], in0=T.ls[:, 192:204], scalar1=4.0, scalar2=float(i), op0=MULT, op1=ADD))
+    need("Y", tok, t_of)
+    for k in (1, 2, 3):
+        t_off = dma("d_off", Y.dma_start(out=T.of[32 * k:32 * k + 32, 0:SN + 36], in_=T.of[0:32, 0:SN + 36]))
+
+    lands = {lot: 0 for lot in LOTS}
+
+    def codes(name, lot, es):
+        j, c0, c1 = PIECES[name]
+        need("g", packed[name])
+        lands[lot] += len(es)
+        return (T.c1[:, BASE[j] + c0:BASE[j] + c1].bitcast(U8), T.xsq[:, BASE[j] + c0:BASE[j] + c1].bitcast(U8), rank[j], "a1_" + lot, es)
+
+    def window(lot, w):
+        end = 512 * (list(LOTS).index(lot) + 1)
+        return T.p1[:, end - w:end]
+
+    def planes(lot, es):
+        j, _, c1, w = LOTS[lot]
+        lands[lot] += len(es)
+        return (window(lot, w), T.pl[:, BASE[j] + c1 - w:BASE[j] + c1], rank[j], "a1_" + lot, es)
+
+    send(codes("A", "a", far_eng))
+    send(codes("B", "a", far_eng))
+    send(planes("a", far_eng))
+    send(codes("E", "c", far_eng))
+    send(codes("C", "b", near_eng))
+    send(planes("c", far_eng), planes("b", near_eng))
+    send(codes("D", "d", near_eng[0::2]), planes("d", near_eng[1::2]))
 
     free = {}
-    full = {}
+    made = {}
 
-    def product(i, bank, rhs, plane, n):
-        need("P", t_wq[i // 2])
-        if bank in free: need("P", free[bank])
-        return p(P.matmul_mx(T.ps[:, 512 * bank:512 * bank + n], T.w1q[:, 128 * i:128 * i + 128], T.w1p[:, 128 * i:128 * i + 128], rhs, plane, True, True))
+    def product(bank, w, wp, rhs, plane, n, *toks):
+        need("P", *toks, *free.get(bank, []))
+        return done("ct", P.matmul_mx(T.ps[:, 512 * bank:512 * bank + n], w, wp, rhs, plane, True, True))
 
-    def evacuate(q, i, bank, c0, n, tok):
+    def bring(q, lot, i):
+        while (lot, i) not in made:
+            a, k = PRODUCTS[len(made)]
+            bank, w, wp = len(made) % 8, T.w1q[:, 128 * k:128 * k + 128], T.w1p[:, 128 * k:128 * k + 128]
+            if a == "o":
+                made[a, k] = (bank, 0, NODES, product(bank, w, wp, T.xq[:, :], T.xp[:, :], NODES, t_xq, t_wq[k // 2]))
+            else:
+                j, c0, c1, _ = LOTS[a]
+                made[a, k] = (bank, NODES + C1 * rank[j] + c0, c1 - c0,
+                              product(bank, w, wp, T.c1[:, BASE[j] + c0:BASE[j] + c1], window(a, c1 - c0), c1 - c0, ("a1_" + a, lands[a])))
+        bank, c0, n, tok = made[lot, i]
         src, dst = T.ps[:, 512 * bank:512 * bank + n], R[i][:, c0:c0 + n]
         need(q, tok)
         if q == "V":
-            free[bank] = v(V.tensor_scalar(out=dst, in0=src, scalar1=0.0, scalar2=0.05, op0=MAX, op1=MULT))
+            tok = v(V.tensor_scalar(out=dst, in0=src, scalar1=0.0, scalar2=0.05, op0=MAX, op1=MULT))
         else:
-            free[bank] = s(S.activation(out=dst, in_=src, func=RELU, scale=0.05))
-        full.setdefault(i, []).append(free[bank])
+            tok = done("cs", S.activation(out=dst, in_=src, func=RELU, scale=0.05))
+        free[bank] = [tok]
+        full[i].append(tok)
 
-    need("P", t_xq)
-    mm = CFG["mm"].split()
-    made = {}
+    for q in "VS":
+        need(q, *full[3])
+    for i in range(3):
+        bring("S", "o", i)
+    next(compose)
+    bring("V", "o", 3)
+    next(compose)
+    bring("S", "a", 0); bring("V", "a", 1)
+    t_oc = next(compose)
+    bring("S", "a", 2); bring("V", "a", 3)
+    for i, q in enumerate("SVSS"):
+        bring(q, "b", i)
+    for i in (0, 1):
+        bring("V", "c", i); bring("V", "d", i)
 
-    def bring(q, name):
-        while name not in made:
-            n = len(made)
-            i = int(mm[n][1])
-            assert n < 8 or mm[n - 8] in brought
-            if mm[n][0] == "o":
-                made[mm[n]] = (n % 8, 0, NODES, product(i, n % 8, T.xq[:, :], T.xp[:, :], NODES))
-            else:
-                k = "abcd".index(mm[n][0])
-                j, c0, c1, w = DV[k]
-                need("P", ("a1_%d" % k, lands[k]))
-                made[mm[n]] = (n % 8, NODES + C1 * order[j] + c0, c1 - c0,
-                               product(i, n % 8, T.c1[:, C1 * j + c0:C1 * j + c1], T.p1[:, NODES * (k + 1) - (c1 - c0):NODES * (k + 1)], c1 - c0))
-        evacuate(q, int(name[1]), *made[name])
-        brought.append(name)
-    brought = []
-
-    M = [T["m%d" % i] for i in range(4)]
-    A = {2: T.a2, 3: T.a3}
-    last = {}
-    piece = {"": (0, 512), "a": (0, 256), "b": (256, 512), "c": (256, 384), "d": (384, 512), "e": (0, 128), "f": (128, 256), "h": (0, 384), "i": (128, 512)}
+    M = {0: T.m0, 1: T.m1, 3: T.m3}
 
     def src(i, c0, c1): return R[i][:, 0:W1T].indirect(T.of[:, c0:c1])
-    def res(i, n0, n1): return M[i][:, n0:n1] if i < 2 else M[i][:, 4 * n0 + 3:4 * n1:4]
-    def on(i, n0, n1): return [t for (a, b, c), t in last.items() if a == i and b < n1 and n0 < c]
+    def in_h(i, n0, n1): return T.h[:, H0 + 4 * n0 + i:H0 + 4 * n1:4]
 
-    def first(q, i, n0, n1):
-        last[i, n0, n1] = move(q, res(i, n0, n1), src(i, 16 + n0 // 16, 16 + n1 // 16), t_off, t_r, t_m2, *full[i])
+    def first(i, n0, n1):
+        return move("S", M[i][:, n0:n1], src(i, 16 + n0 // 16, 16 + n1 // 16), t_off, *full[i])
 
-    def more(i, e, n0, n1, out=None):
-        need("V", t_off, *on(i, n0, n1), *full[i])
-        last[i, n0, n1] = v(V.tensor_tensor(out=res(i, n0, n1) if out is None else out, in0=src(i, BY * e + 16 + n0 // 16, BY * e + 16 + n1 // 16), in1=res(i, n0, n1), op=MAX))
-        return last[i, n0, n1]
+    def more(i, e, n0, n1, *toks):
+        need("V", t_off, *toks)
+        return v(V.tensor_tensor(out=in_h(i, n0, n1) if e == 3 else M[i][:, n0:n1], in1=M[i][:, n0:n1], op=MAX,
+                                 in0=src(i, BY * e + 16 + n0 // 16, BY * e + 16 + n1 // 16)))
 
     def four(i, n0, n1):
-        last[i, n0, n1] = move("S", A[i][:, 4 * n0:4 * n1], src(i, NAT + n0 // 4, NAT + n1 // 4), t_off, t_r, *full[i])
+        return move("S", (T.a2, T.a3)[i - 2][:, 4 * n0:4 * n1], src(i, NAT + n0 // 4, NAT + n1 // 4), t_off, *full[i])
 
-    scans = []
+    def scan(o, i, n, tok):
+        need("V", tok, t_mask)
+        return v(V.tensor_tensor_scan(o, T.mask[:, 0:n], i, 0.0, MULT, MAX))
 
-    def scan(i, n0, n1, out=None):
-        need("V", *on(i, n0, n1), t_mask)
-        last[i, n0, n1] = v(V.tensor_tensor_scan(M[i][:, 4 * n0:4 * n1] if out is None else out, T.mask[:, 0:4 * (n1 - n0)], A[i][:, 4 * n0:4 * n1], 0.0, MULT, MAX))
-        scans.append(last[i, n0, n1])
-        return last[i, n0, n1]
+    def listed(q, i, *toks):
+        return move(q, T.hs[:, i:768:4], T.h[:, H0:H0 + 2048].indirect(T.of[:, SN + 12 * i:SN + 12 * i + 12]), t_h0, *toks)
 
-    def slots(q, i, c0, c1):
-        c = SN if i < 2 else SN4
-        return move(q, T.hs[:, 64 * c0 + i:64 * c1:4], M[i][:, :].indirect(T.of[:, c + c0:c + c1]), *on(i, 0, NODES))
+    t0 = first(0, 0, NODES)
+    bring("V", "c", 2); bring("V", "d", 2)
+    t1 = first(1, 0, NODES)
+    t2 = [four(2, 0, 256), four(2, 256, NODES)]
+    bring("S", "c", 3); bring("V", "d", 3)
+    for e in range(4):
+        tb = move("S", T.b3[:, e:768:4], src(3, OC + 12 * e, OC + 12 * e + 12), t_oc, *full[3])
+    t3 = first(3, 256, NODES)
+    for e in (1, 2):
+        t0 = more(0, e, 0, NODES, t0, *full[0])
+        t1 = more(1, e, 0, NODES, t1, *full[1])
+    t2 = [scan(T.h[:, H0 - 1 + 1024 * k:H0 + 1023 + 1024 * k], T.a2[:, 1024 * k:1024 * k + 1024], 1024, t2[k]) for k in range(2)]
+    th = [more(0, 3, 0, 256, t2[0], t0), more(1, 3, 0, NODES, t2[1], t1), more(0, 3, 256, NODES, t2[1])]
+    tb = scan(T.t3[:, :], T.b3[:, :], 768, tb)
+    t_hs = [listed("S", 1, *th), listed("V", 0, *th), move("V", T.hs[:, 3:768:4], T.t3[:, 3:768:4], tb), listed("S", 2, *th)]
+    ta = [four(3, 0, 128), four(3, 128, 256)]
+    t_w2q = quantise(T.w2q[:, :], T.w2p[:, :], T.w2b[:, :], t_w2)
 
+    need("g", quantise(T.hsq[:, :], T.pl[:, HS:HS + 3 * C2], T.hs[:, :], *t_hs))
+    half = len(far_eng) // 2
+    eng = dict(zip(rank, (far_eng[:half], far_eng[half:], near_eng)))
+    there = {d: slice(C2 * slot(r, d), C2 * slot(r, d) + C2) for d in rank}
+    send(*[(T.c2[:, there[d]].bitcast(U8), T.hsq[:, C2 * slot(d, r):C2 * slot(d, r) + C2].bitcast(U8), d, "a2", eng[d]) for d in rank])
+    send(*[(T.p2[:, there[d]], T.pl[:, HS + C2 * slot(d, r):HS + C2 * slot(d, r) + C2], d, "a2", eng[d]) for d in rank])
 
-    parts = []
-    quarter, half = len(far_eng) // 4, len(near_eng) // 2
-    engs = {far[0]: (far_eng[:quarter], far_eng[quarter:2 * quarter]), far[1]: (far_eng[2 * quarter:3 * quarter], far_eng[3 * quarter:]),
-            near[0]: (near_eng[:half], near_eng[half:])}
-    for d in order:
-        c0 = C2 * slot(d, r)
-        a = r - pair(d)
-        codes = T.c2[:, C2 * a:C2 * a + C2] if a in (0, 1) else T.hq[:, NODES:NODES + C2]
-        plane = T.p2[:, PW * a:PW * a + PW] if a in (0, 1) else T.hp[:, NODES:NODES + PW]
-        w0 = HS + c0 - (PW - C2 if a == 0 else 0)
-        parts.append((codes.bitcast(U8), T.hsq[:, c0:c0 + C2].bitcast(U8), d, "a2", engs[d][0]))
-        parts.append((plane, T.pl[:, w0:w0 + PW], d, "a2", engs[d][1]))
+    def own(bank, n0, n1, *toks):
+        tok = quantise(T.hq[:, n0:n1], T.hp[:, n0:n1], T.h[:, H0 + 4 * n0:H0 + 4 * n1], *toks)
+        return product(bank, T.w2q[:, :], T.w2p[:, :], T.hq[:, n0:n1], T.hp[:, n0:n1], n1 - n0, tok, t_w2q)
 
-    def send2(tok):
-        need("g", tok)
-        send(parts)
-    t_a2 = ("a2", len(far_eng) + len(near_eng))
+    tc = [t3, t3]
+    for e in (1, 2):
+        tc = [more(3, e, 256 + 128 * k, 384 + 128 * k, tc[k], *full[3]) for k in range(2)]
+    ta[0] = scan(T.s3[:, 0:512], T.a3[:, 0:512], 512, ta[0])
+    tc = more(3, 3, 256, NODES, *tc, *t_hs)
+    ta[1] = scan(T.s3[:, 512:1024], T.a3[:, 512:1024], 512, ta[1])
+    ta[0] = move("S", in_h(3, 0, 128), T.s3[:, 3:512:4], ta[0], *t_hs)
+    pb = own(4, 256, NODES, tc)
+    ta[1] = move("V", in_h(3, 128, 256), T.s3[:, 515:1024:4], ta[1])
+    pa = [own(5 + k, 128 * k, 128 * k + 128, ta[k]) for k in range(2)]
+    t_tab = [move("V", T.u[:, 256:NODES], T.ps[:, 2048:2304], pb), move("S", T.u[:, 0:128], T.ps[:, 2560:2688], pa[0]),
+             move("V", T.u[:, 128:256], T.ps[:, 3072:3200], pa[1])]
 
-    def product2(bank, rhs, plane, n):
-        need("P", free[bank], st["w2q"])
-        return p(P.matmul_mx(T.ps[:, 512 * bank:512 * bank + n], T.w2q[:, :], T.w2p[:, :], rhs, plane, True, True))
-    def via(i, e): return src(i, OC + 12 * e, OC + 12 * e + 12)
-    def inh(n0, n1): return [t for (b, c, t) in into if b < n1 and n0 < c]
-
-    t_hs, into, t_own, t_tab = [], [], {}, []
-    for w in CFG["work"].split():
-        if w[0] in "oabcd": bring(w[2], w[:2])
-        elif w[0] == "f": first("S", int(w[1]), *piece[w[2:]])
-        elif w[0] == "F": first("V", int(w[1]), *piece[w[2:]])
-        elif w[0] == "g": four(int(w[1]), *piece[w[2:]])
-        elif w[0] == "m": more(int(w[1]), int(w[2]), *piece[w[3:]])
-        elif w[0] == "s": scan(int(w[1]), *piece[w[2:]])
-        elif w[0] == "z":
-            n0, n1 = piece[w[2:]]
-            i = int(w[1])
-            into.append((n0, n1, scan(i, n0, n1, T.h[:, H0 + i - 3 + 4 * n0:H0 + i - 3 + 4 * n1])))
-        elif w[0] == "H":
-            i, (c0, c1) = int(w[2]), {"": (0, 12), "a": (0, 6), "b": (6, 12)}[w[3:]]
-            t_hs.append(move(w[1], T.hs[:, 64 * c0 + i:64 * c1:4], T.h[:, H0:H0 + 2048].indirect(T.of[:, SN + 12 * i + c0:SN + 12 * i + c1]),
-                             t_h0, *inh(0, NODES), *[st[z] for z in "Z" if z in st and (w[1] == "S" or CFG["waw"])]))
-            st["H"] = list(t_hs)
-        elif w[0] == "M":
-            i, (n0, n1) = int(w[1]), piece[w[3:]]
-            need("V", *[t for t in inh(n0, n1 + (i == 3)) if t in scans], *st.get("H", []))
-            into.append((n0, n1, more(i, int(w[2]), n0, n1, T.h[:, H0 + 4 * n0 + i:H0 + 4 * n1:4])))
-        elif w[0] == "i":
-            i, (n0, n1) = int(w[2]), piece[w[3:]]
-            clob = [t for t in inh(n0, n1 + (i == 3)) if t in scans]
-            into.append((n0, n1, move(w[1], T.h[:, H0 + 4 * n0 + i:H0 + 4 * n1:4], res(i, n0, n1), *on(i, n0, n1), *clob, *st.get("H", []))))
-        elif w[0] == "h":
-            n0, n1 = piece[w[1:]]
-            need("V", *inh(n0, n1))
-            t_h = v(V.quantize_mx(out=T.hq[:, n0:n1], scales=T.hp[:, n0:n1], in_=T.h[:, H0 + 4 * n0:H0 + 4 * n1]))
-            need("P", t_h)
-            bank = 4 + len(t_own)
-            t_own[w[1:]] = (bank, product2(bank, T.hq[:, n0:n1], T.hp[:, n0:n1], n1 - n0))
-        elif w[0] == "u":
-            (n0, n1), (bank, tok) = piece[w[2:]], t_own[w[2:]]
-            t_tab.append(move(w[1], T.u[:, n0:n1], T.ps[:, 512 * bank:512 * bank + n1 - n0], tok))
-        elif w == "T": t_u = v(V.memset(T.u[:, NODES + C2 * r:NODES + C2 * r + C2], 0.0))
-        elif w == "U":
-            if "T" not in CFG["work"]: t_u = v(V.memset(T.u[:, NODES + C2 * r:NODES + C2 * r + C2], 0.0))
-            need("V", t_w2)
-            st["w2q"] = v(V.quantize_mx(out=T.w2q[:, :], scales=T.w2p[:, :], in_=T.w2b[:, :]))
-        elif w == "Q":
-            need("V", *t_hs)
-            send2(v(V.quantize_mx(out=T.hsq[:, :], scales=T.pl[:, HS:HS + 3 * C2], in_=T.hs[:, :])))
-        elif w[0] == "k": compose(w)
-        elif w[0] == "n":
-            i, e = int(w[1]), int(w[2])
-            if e == 0:
-                st["n", i] = move("S", T.b1[:, i - 2, :], via(i, 0), st["oc"], t_r, *full[i])
-            else:
-                need("V", st["n", i], st["oc"], *full[i])
-                st["n", i] = v(V.tensor_tensor(out=T.hs[:, i:768:4] if e == 3 else T.b1[:, i - 2, :], in0=via(i, e), in1=T.b1[:, i - 2, :], op=MAX))
-                if e == 3: t_hs.append(st["n", i])
-        elif w == "N":
-            for e in range(4):
-                st["N"] = move("S", T.b4[:, e:768:4], via(3, e), st["oc"], t_r, *full[3])
-        elif w == "Z":
-            need("V", st["N"], t_mask)
-            st["Z"] = v(V.tensor_tensor_scan(T.hs[:, :], T.mask[:, 0:768], T.b4[:, :], 0.0, MULT, MAX))
-            t_hs.append(st["Z"])
-        else:
-            need(w[0], *[st[z] for z in "Z" if z in st])
-            t_hs.append(slots(w[0], int(w[1]), *{"": (0, 12), "a": (0, 6), "b": (6, 12)}[w[2:]]))
-    need("P", t_a2)
-    ta = product2(2, T.c2[:, :], T.p2[:, PW - C2:PW + C2], 2 * C2)
-    tb = product2(3, T.hq[:, NODES - C2:NODES + C2], T.hp[:, NODES - C2:NODES + C2], 2 * C2)
-    a = pair(r)
+    a = min(d for d in others if d + 1 in others)
     b = [d for d in others if d not in (a, a + 1)][0]
-    t_tab.append(move("V", T.u[:, NODES + C2 * a:NODES + C2 * (a + 2)], T.ps[:, 1024:1024 + 2 * C2], ta))
-    t_tab.append(move("S", T.u[:, NODES + C2 * b:NODES + C2 * (b + 1)], T.ps[:, 1536 + C2:1536 + 2 * C2], tb))
+    ca, cb = C2 * slot(a, r), C2 * (b > a)
+    landed = ("a2", 2 * (len(far_eng) + len(near_eng)))
+    pb = product(3, T.w2q[:, :], T.w2p[:, :], T.c2[:, cb:cb + 2 * C2], T.p2[:, cb:cb + 2 * C2], 2 * C2, landed)
+    pa = product(2, T.w2q[:, :], T.w2p[:, :], T.c2[:, ca:ca + 2 * C2], T.p2[:, ca:ca + 2 * C2], 2 * C2)
+    t_tab.append(move("V", T.u[:, NODES + C2 * a:NODES + C2 * (a + 2)], T.ps[:, 1024:1024 + 2 * C2], pa))
+    t_tab.append(move("S", T.u[:, NODES + C2 * b:NODES + C2 * (b + 1)], T.ps[:, 1536 + cb:1536 + cb + C2], pb))
 
-    def tgt(e, c0=0, c1=16): return T.u[:, 0:W2T].indirect(T.of[:, BY * e + c0:BY * e + c1])
-    cuts = CFG["ycuts"]
-    tok = [move(q, T.yb[:, 16 * c0:16 * c1], tgt(0, c0, c1), t_u, *t_tab) for q, c0, c1 in cuts]
-    for w in CFG["yorder"].split():
-        k, e = int(w[0]), int(w[1])
-        _, c0, c1 = cuts[k]
-        need("V", tok[k])
-        tok[k] = v(V.tensor_tensor(out=T.yb[:, 16 * c0:16 * c1], in0=tgt(e, c0, c1), in1=T.yb[:, 16 * c0:16 * c1], op=MAX))
-    for q, c0, c1 in CFG["ystore"]:
-        need(q, *[t for t, (_, a, b) in zip(tok, cuts) if a < c1 and c0 < b])
-        t_y = dma("d_y", queues[q].dma_start(out=T.y[:, 16 * c0:16 * c1], in_=T.yb[:, 16 * c0:16 * c1]))
+    def target(e, k): return T.u[:, 0:W2T].indirect(T.of[:, BY * e + 8 * k:BY * e + 8 * k + 8])
+    yb = [T.yb[:, 128 * k:128 * k + 128] for k in range(2)]
+    tok = [move(q, yb[k], target(0, k), t_u, *t_tab) for k, q in enumerate("VS")]
+    for e in (1, 2, 3):
+        for k in range(2):
+            need("V", tok[k])
+            tok[k] = v(V.tensor_tensor(out=yb[k], in0=target(e, k), in1=yb[k], op=MAX))
+    for k, q in enumerate("YS"):
+        need(q, tok[k])
+        t_y = dma("d_y", queues[q].dma_start(out=T.y[:, 128 * k:128 * k + 128], in_=yb[k]))
 
     need("g", ("sent", count["sent"]))
-    need("Y", t_y, *[(k, count[k]) for k in ("cv", "cs", "ct")])
+    need("Y", *[(k, count[k]) for k in ("cg", "ct", "cs", "cv")], t_y)

from concourse.bass import DstId, RemoteDMATransfer
from concourse.mybir import dt, AluOpType, ActivationFunctionType

N, NODES, TG, C1, C2 = 4, 512, 256, 320, 64
W1T = NODES + N * C1
W2T = NODES + N * C2
F8 = "float8_e4m3fn_x4"
FAR0, FAR1, NEAR = 0, 1, 2
BASE = {FAR0: 0, NEAR: C1, FAR1: 2 * C1}
PIECES = {"A": (FAR0, 0, 128), "B": (FAR0, 128, C1), "C": (NEAR, 0, 192), "D": (NEAR, 192, C1), "E": (FAR1, 0, C1)}
LOTS = {"a": (FAR0, 0, C1, C1), "b": (NEAR, 0, 192, C1), "c": (FAR1, 0, C1, C1), "d": (NEAR, 192, C1, 512)}
PRODUCTS = [(lot, i) for lot in "oab" for i in range(4)] + [("c", 0), ("c", 1), ("d", 0), ("d", 1)] + [(lot, i) for i in (2, 3) for lot in "cd"]
BY, NAT, SN, OC, OFW = 48, 192, 320, 360, 408
H0 = 16
HS = 3 * C1
SCRATCH = {
    "xb": ("sbuf", [128, 2048], "bfloat16"), "xq": ("sbuf", [128, 512], F8), "xp": ("sbuf", [128, 512], "uint8"),
    "w1b": ("sbuf", [128, 2048], "bfloat16"), "w1q": ("sbuf", [128, 512], F8), "w1p": ("sbuf", [128, 512], "uint8"),
    "w2b": ("sbuf", [128, 512], "bfloat16"), "w2q": ("sbuf", [128, 128], F8), "w2p": ("sbuf", [128, 128], "uint8"),
    "xs": ("sbuf", [128, 12 * C1], "bfloat16"), "xsq": ("sbuf", [128, 3 * C1], F8),
    "hs": ("sbuf", [128, 12 * C2], "bfloat16"), "hsq": ("sbuf", [128, 3 * C2], F8),
    "pl": ("sbuf", [128, 3 * C1 + 3 * C2], "uint8"),
    "c1": ("sbuf", [128, 3 * C1], F8), "p1": ("sbuf", [128, 4 * 512], "uint8"),
    "c2": ("sbuf", [128, 3 * C2], F8), "p2": ("sbuf", [128, 3 * C2], "uint8"),
    "r0": ("sbuf", [128, W1T], "bfloat16"), "r1": ("sbuf", [128, W1T], "bfloat16"),
    "r2": ("sbuf", [128, W1T], "bfloat16"), "r3": ("sbuf", [128, W1T], "bfloat16"),
    "m0": ("sbuf", [128, 512], "bfloat16"), "m1": ("sbuf", [128, 512], "bfloat16"), "m3": ("sbuf", [128, 512], "bfloat16"),
    "a2": ("sbuf", [128, 2048], "bfloat16"), "a3": ("sbuf", [128, 1024], "bfloat16"), "s3": ("sbuf", [128, 1024], "bfloat16"),
    "b3": ("sbuf", [128, 768], "bfloat16"), "t3": ("sbuf", [128, 768], "bfloat16"), "mask": ("sbuf", [128, 1024], "bfloat16"),
    "h": ("sbuf", [128, H0 + 2048], "bfloat16"), "hq": ("sbuf", [128, 512], F8), "hp": ("sbuf", [128, 512], "uint8"),
    "u": ("sbuf", [128, W2T], "float32"), "yb": ("sbuf", [128, TG], "float32"),
    "sl": ("sbuf", [128, 80], "int32"), "so": ("sbuf", [128, 320], "uint16"),
    "ls": ("sbuf", [32, 204], "int32"), "lc": ("sbuf", [16, 192], "uint16"), "of": ("sbuf", [128, OFW], "uint16"),
    "s4": ("sbuf", [32, 12], "int32"), "k1": ("sbuf", [32, 12], "int32"), "k2": ("sbuf", [32, 12], "float32"),
    "k3": ("sbuf", [32, 12], "float32"), "ko": ("sbuf", [128, 12], "uint16"), "bye": ("sbuf", [128, 512], "int32"),
    "ga": ("sbuf", [128, 192], "float32"), "gt": ("sbuf", [32, 192], "float32"), "oc": ("sbuf", [16, 48], "uint16"),
    "ps": ("psum", [128, 4096], "float32"),
}
SEMAPHORES = ["cg", "cv", "cs", "ct", "d_snd", "d_ls", "d_x", "d_s2", "d_w0", "d_w1", "d_w2", "d_of", "d_off", "d_bye", "d_s4",
              "d_oc", "d_y", "a1_a", "a1_b", "a1_c", "a1_d", "a2", "sent"]


def rank_program(g, core, T, topo):
    r = T.rank_of(core)
    if r is None:
        return
    V, S, P, Y = g.vector, g.scalar, g.tensor, g.sync
    queues = {"g": g, "V": V, "S": S, "P": P, "Y": Y}
    MAX, MULT, ADD = AluOpType.max, AluOpType.mult, AluOpType.add
    COPY, RELU = ActivationFunctionType.Copy, ActivationFunctionType.Relu
    U8 = dt.uint8
    count = {}
    seen = {}

    def done(sem, ins, k=1):
        ins.then_inc(T.sem[sem], k)
        count[sem] = count.get(sem, 0) + k
        return (sem, count[sem])

    def need(q, *toks):
        most = {}
        for sem, k in toks:
            most[sem] = max(k, most.get(sem, 0))
        for sem, k in most.items():
            if seen.get((q, sem), 0) < k:
                queues[q].wait_ge(T.sem[sem], k)
                seen[(q, sem)] = k

    def v(ins): return done("cv", ins)
    def dma(sem, ins): return done(sem, ins, 16)

    def move(q, o, i, *toks):
        need(q, *toks)
        return v(V.tensor_copy(out=o, in_=i)) if q == "V" else done("cs", S.activation(out=o, in_=i, func=COPY))

    def quantise(codes, plane, tile, *toks):
        need("V", *toks)
        return v(V.quantize_mx(out=codes, scales=plane, in_=tile))

    def zeros(ap, n): return done("cg", g.iota(ap, [[0, n]], 0, 0, allow_small_or_imprecise_dtypes=True))

    others = [d for d in range(N) if d != r]
    me = T.cores[r]
    far = [d for d in others if topo.chip(T.cores[d]) != topo.chip(me)]
    far.sort(key=lambda d: topo.die(T.cores[d]) != topo.die(me))
    rank = far + [d for d in others if d not in far]
    far_eng = topo.engines(me, T.cores[rank[FAR0]])
    near_eng = [e for e in topo.engines(me, T.cores[rank[NEAR]]) if e not in far_eng]

    def slot(a, b): return a - (1 if a > b else 0)
    runs = []
    for d in others:
        if runs and runs[-1][0] + runs[-1][1] == d: runs[-1][1] += 1
        else: runs.append([d, 1])

    def send(*parts):
        ts = []
        for o, i, d, sm, es in parts:
            rid, pid, _ = topo.addr(T.cores[d])
            ts.append(RemoteDMATransfer(dst_ids=[DstId(rid=rid, pnc=pid)], dma_engine_mask=sum(1 << e for e in es), remote_sem=T.sem[sm], src=i, dst=o))
            count["sent"] = count.get("sent", 0) + len(es)
        g.remote_dma_fused(ts, local_sem=T.sem.sent)

    dma("d_snd", Y.dma_start(out=T.sl[0:16, :], in_=T.snd1[:, :]))
    t_snd = dma("d_snd", S.dma_start(out=T.sl[16:32, :], in_=T.snd1[:, :]))
    dma("d_x", S.dma_start(out=T.xb[64:128, :], in_=T.x[64:128, :]))
    t_x = dma("d_x", Y.dma_start(out=T.xb[0:64, :], in_=T.x[0:64, :]))
    dma("d_ls", Y.dma_start(out=T.ls[0:16, 64:192], in_=T.src1[:, :]))
    t_ls = dma("d_ls", S.dma_start(out=T.ls[0:16, 0:64], in_=T.src2[:, :]))
    dma("d_s2", S.dma_start(out=T.ls[16:32, 64:192], in_=T.src1[:, :]))
    for k, q in enumerate((Y, S)):
        c = 192
        for d, n in runs:
            t_s2 = dma("d_s2", q.dma_start(out=T.ls[16 * k:16 * k + 16, c:c + 4 * n], in_=T.snd2[:, 4 * d:4 * d + 4 * n]))
            c += 4 * n
    t_w1 = [dma("d_w%d" % k, Y.dma_start(out=T.w1b[:, 1024 * k:1024 * k + 1024], in_=T.w1[:, 1024 * k:1024 * k + 1024])) for k in range(2)]
    t_w2 = dma("d_w2", Y.dma_start(out=T.w2b[:, :], in_=T.w2[:, :]))

    R = [T.r0, T.r1, T.r2, T.r3]
    gap = [t[:, NODES + C1 * r:NODES + C1 * r + C1] for t in R]
    t_s4 = v(V.memset(T.s4[:, :], 0))
    t_ko = v(V.memset(T.ko[:, :], 0))
    t_h0 = v(V.memset(T.h[:, H0 + 2047:H0 + 2048], 0.0))
    t_one = v(V.memset(T.mask[:, :], 1.0))
    full = {i: [v(V.memset(gap[i], 0.0))] for i in (0, 1)}
    t_bye = done("cg", g.iota(T.bye[:, :], [[0, 512]], 0, 0))
    t_u = zeros(T.u[:, NODES + C2 * r:NODES + C2 * r + C2], C2)
    for i in (2, 3):
        full[i] = [zeros(gap[i], C1)]
    need("Y", t_bye, t_s4, t_ko)
    for k in range(2):
        for a in range(4):
            t_bye = dma("d_bye", Y.dma_start(out=T.bye[16 * k:16 * k + 4, 128 * a:128 * a + 128], in_=T.src1[4 * a:4 * a + 4, :]))
        c = 0
        for d, n in runs:
            c0 = k if c == 0 else 0
            t_s4 = dma("d_s4", Y.dma_start(out=T.s4[16 * k:16 * k + 16, c + c0 - k:c + 4 * n - k], in_=T.snd2[:, 4 * d + c0:4 * d + 4 * n]))
            c += 4 * n

    need("V", t_snd)
    for k in (1, 2, 3):
        tok = v(V.tensor_copy(out=T.sl[32 * k:32 * k + 32, :], in_=T.sl[0:32, :]))
    need("V", t_one)
    t_mask = v(V.memset(T.mask[:, 0::4], 0.0))
    need("V", tok)
    t_so = {}
    for t in (2, 0, 3, 1):
        t_so[t] = v(V.tensor_scalar(out=T.so[:, 80 * t:80 * t + 80], in0=T.sl[:, :], scalar1=4.0, scalar2=float(t), op0=MULT, op1=ADD))

    def by_source(*blocks):
        need("V", t_ls)
        for q in blocks:
            need("Y", v(V.tensor_copy(out=T.lc[:, BY * q:BY * q + BY], in_=T.ls[0:16, q:192:4])))
            for k in range(2):
                tok = dma("d_of", Y.dma_start(out=T.of[16 * k + 4 * q:16 * k + 4 * q + 4, 0:NAT], in_=T.lc[:, BY * q:BY * q + BY]))
        return tok

    def composing():
        need("V", t_s4, t_ko)
        tok = v(V.tensor_scalar(out=T.k1[:, :], in0=T.s4[:, :], scalar1=2, scalar2=None, op0=AluOpType.arith_shift_right))
        yield None
        need("V", tok)
        tok = v(V.tensor_scalar(out=T.k2[:, :], in0=T.k1[:, :], scalar1=-511 / 128, scalar2=None, op0=MULT))
        yield None
        need("V", tok)
        tok = v(V.tensor_tensor(out=T.k3[:, :], in0=T.s4[:, :], in1=T.k2[:, :], op=ADD))
        yield None
        need("V", tok)
        tok = v(V.tensor_scalar(out=T.ko[0:32, :], in0=T.k3[:, :], scalar1=128.0, scalar2=None, op0=MULT))
        yield None
        tok = move("V", T.ga[:, :], T.bye[:, 0:512].indirect(T.ko[:, :]), tok, t_bye)
        yield None
        need("V", tok)
        tok = v(V.transpose(out=T.gt[:, :], in_=T.ga[0:32, :]))
        yield None
        need("V", tok)
        for e in range(4):
            tok = v(V.tensor_copy(out=T.oc[:, 12 * e:12 * e + 12], in_=T.gt[0:16, e:192:16]))
        need("Y", tok)
        for k in range(8):
            tok = dma("d_oc", Y.dma_start(out=T.of[16 * k:16 * k + 16, OC:OC + 48], in_=T.oc[:, :]))
        yield tok
    compose = composing()

    gathered, packed = {}, {}

    def gather(name, engines):
        j, c0, c1 = PIECES[name]
        gathered[name] = []
        for t, q in enumerate(engines):
            o = 80 * t + 20 * rank[j]
            gathered[name].append(move(q, T.xs[:, 4 * (BASE[j] + c0) + t:4 * (BASE[j] + c1):4],
                                       T.xb[:, 0:2048].indirect(T.so[:, o + c0 // 16:o + c1 // 16]), t_x, t_so[t]))

    def pack(name):
        j, c0, c1 = PIECES[name]
        c0, c1 = BASE[j] + c0, BASE[j] + c1
        packed[name] = quantise(T.xsq[:, c0:c1], T.pl[:, c0:c1], T.xs[:, 4 * c0:4 * c1], *gathered[name])

    def weights(k): return quantise(T.w1q[:, 256 * k:256 * k + 256], T.w1p[:, 256 * k:256 * k + 256], T.w1b[:, 1024 * k:1024 * k + 1024], t_w1[k])

    gather("A", "VVSS"); by_source(0, 1); pack("A")
    gather("B", "VVSS"); t_of = by_source(2, 3); pack("B")
    gather("E", "VSSS")
    t_xq = quantise(T.xq[:, :], T.xp[:, :], T.xb[:, :], t_x)
    pack("E")
    gather("C", "VSSS")
    t_wq = [weights(0)]
    next(compose)
    pack("C")
    next(compose)
    gather("D", "SSSS")
    t_wq.append(weights(1))
    next(compose)
    pack("D")
    next(compose)
    need("V", t_s2, t_ls)
    v(V.tensor_copy(out=T.of[0:32, NAT:SN], in_=T.ls[:, 64:192]))
    for i in range(3):
        tok = v(V.tensor_scalar(out=T.of[0:32, SN + 12 * i:SN + 12 * i + 12], in0=T.ls[:, 192:204], scalar1=4.0, scalar2=float(i), op0=MULT, op1=ADD))
    need("Y", tok, t_of)
    for k in (1, 2, 3):
        t_off = dma("d_off", Y.dma_start(out=T.of[32 * k:32 * k + 32, 0:SN + 36], in_=T.of[0:32, 0:SN + 36]))

    lands = {lot: 0 for lot in LOTS}

    def codes(name, lot, es):
        j, c0, c1 = PIECES[name]
        need("g", packed[name])
        lands[lot] += len(es)
        return (T.c1[:, BASE[j] + c0:BASE[j] + c1].bitcast(U8), T.xsq[:, BASE[j] + c0:BASE[j] + c1].bitcast(U8), rank[j], "a1_" + lot, es)

    def window(lot, w):
        end = 512 * (list(LOTS).index(lot) + 1)
        return T.p1[:, end - w:end]

    def planes(lot, es):
        j, _, c1, w = LOTS[lot]
        lands[lot] += len(es)
        return (window(lot, w), T.pl[:, BASE[j] + c1 - w:BASE[j] + c1], rank[j], "a1_" + lot, es)

    send(codes("A", "a", far_eng))
    send(codes("B", "a", far_eng))
    send(planes("a", far_eng))
    send(codes("E", "c", far_eng))
    send(codes("C", "b", near_eng))
    send(planes("c", far_eng), planes("b", near_eng))
    send(codes("D", "d", near_eng[0::2]), planes("d", near_eng[1::2]))

    free = {}
    made = {}

    def product(bank, w, wp, rhs, plane, n, *toks):
        need("P", *toks, *free.get(bank, []))
        return done("ct", P.matmul_mx(T.ps[:, 512 * bank:512 * bank + n], w, wp, rhs, plane, True, True))

    def bring(q, lot, i):
        while (lot, i) not in made:
            a, k = PRODUCTS[len(made)]
            bank, w, wp = len(made) % 8, T.w1q[:, 128 * k:128 * k + 128], T.w1p[:, 128 * k:128 * k + 128]
            if a == "o":
                made[a, k] = (bank, 0, NODES, product(bank, w, wp, T.xq[:, :], T.xp[:, :], NODES, t_xq, t_wq[k // 2]))
            else:
                j, c0, c1, _ = LOTS[a]
                made[a, k] = (bank, NODES + C1 * rank[j] + c0, c1 - c0,
                              product(bank, w, wp, T.c1[:, BASE[j] + c0:BASE[j] + c1], window(a, c1 - c0), c1 - c0, ("a1_" + a, lands[a])))
        bank, c0, n, tok = made[lot, i]
        src, dst = T.ps[:, 512 * bank:512 * bank + n], R[i][:, c0:c0 + n]
        need(q, tok)
        if q == "V":
            tok = v(V.tensor_scalar(out=dst, in0=src, scalar1=0.0, scalar2=0.05, op0=MAX, op1=MULT))
        else:
            tok = done("cs", S.activation(out=dst, in_=src, func=RELU, scale=0.05))
        free[bank] = [tok]
        full[i].append(tok)

    for q in "VS":
        need(q, *full[3])
    for i in range(3):
        bring("S", "o", i)
    next(compose)
    bring("V", "o", 3)
    next(compose)
    bring("S", "a", 0); bring("V", "a", 1)
    t_oc = next(compose)
    bring("S", "a", 2); bring("V", "a", 3)
    for i, q in enumerate("SVSS"):
        bring(q, "b", i)
    for i in (0, 1):
        bring("V", "c", i); bring("V", "d", i)

    M = {0: T.m0, 1: T.m1, 3: T.m3}

    def src(i, c0, c1): return R[i][:, 0:W1T].indirect(T.of[:, c0:c1])
    def in_h(i, n0, n1): return T.h[:, H0 + 4 * n0 + i:H0 + 4 * n1:4]

    def first(i, n0, n1):
        return move("S", M[i][:, n0:n1], src(i, 16 + n0 // 16, 16 + n1 // 16), t_off, *full[i])

    def more(i, e, n0, n1, *toks):
        need("V", t_off, *toks)
        return v(V.tensor_tensor(out=in_h(i, n0, n1) if e == 3 else M[i][:, n0:n1], in1=M[i][:, n0:n1], op=MAX,
                                 in0=src(i, BY * e + 16 + n0 // 16, BY * e + 16 + n1 // 16)))

    def four(i, n0, n1):
        return move("S", (T.a2, T.a3)[i - 2][:, 4 * n0:4 * n1], src(i, NAT + n0 // 4, NAT + n1 // 4), t_off, *full[i])

    def scan(o, i, n, tok):
        need("V", tok, t_mask)
        return v(V.tensor_tensor_scan(o, T.mask[:, 0:n], i, 0.0, MULT, MAX))

    def listed(q, i, *toks):
        return move(q, T.hs[:, i:768:4], T.h[:, H0:H0 + 2048].indirect(T.of[:, SN + 12 * i:SN + 12 * i + 12]), t_h0, *toks)

    t0 = first(0, 0, NODES)
    bring("V", "c", 2); bring("V", "d", 2)
    t1 = first(1, 0, NODES)
    t2 = [four(2, 0, 256), four(2, 256, NODES)]
    bring("S", "c", 3); bring("V", "d", 3)
    for e in range(4):
        tb = move("S", T.b3[:, e:768:4], src(3, OC + 12 * e, OC + 12 * e + 12), t_oc, *full[3])
    t3 = first(3, 256, NODES)
    for e in (1, 2):
        t0 = more(0, e, 0, NODES, t0, *full[0])
        t1 = more(1, e, 0, NODES, t1, *full[1])
    t2 = [scan(T.h[:, H0 - 1 + 1024 * k:H0 + 1023 + 1024 * k], T.a2[:, 1024 * k:1024 * k + 1024], 1024, t2[k]) for k in range(2)]
    th = [more(0, 3, 0, 256, t2[0], t0), more(1, 3, 0, NODES, t2[1], t1), more(0, 3, 256, NODES, t2[1])]
    tb = scan(T.t3[:, :], T.b3[:, :], 768, tb)
    t_hs = [listed("S", 1, *th), listed("V", 0, *th), move("V", T.hs[:, 3:768:4], T.t3[:, 3:768:4], tb), listed("S", 2, *th)]
    ta = [four(3, 0, 128), four(3, 128, 256)]
    t_w2q = quantise(T.w2q[:, :], T.w2p[:, :], T.w2b[:, :], t_w2)

    need("g", quantise(T.hsq[:, :], T.pl[:, HS:HS + 3 * C2], T.hs[:, :], *t_hs))
    half = len(far_eng) // 2
    eng = dict(zip(rank, (far_eng[:half], far_eng[half:], near_eng)))
    there = {d: slice(C2 * slot(r, d), C2 * slot(r, d) + C2) for d in rank}
    send(*[(T.c2[:, there[d]].bitcast(U8), T.hsq[:, C2 * slot(d, r):C2 * slot(d, r) + C2].bitcast(U8), d, "a2", eng[d]) for d in rank])
    send(*[(T.p2[:, there[d]], T.pl[:, HS + C2 * slot(d, r):HS + C2 * slot(d, r) + C2], d, "a2", eng[d]) for d in rank])

    def own(bank, n0, n1, *toks):
        tok = quantise(T.hq[:, n0:n1], T.hp[:, n0:n1], T.h[:, H0 + 4 * n0:H0 + 4 * n1], *toks)
        return product(bank, T.w2q[:, :], T.w2p[:, :], T.hq[:, n0:n1], T.hp[:, n0:n1], n1 - n0, tok, t_w2q)

    tc = [t3, t3]
    for e in (1, 2):
        tc = [more(3, e, 256 + 128 * k, 384 + 128 * k, tc[k], *full[3]) for k in range(2)]
    ta[0] = scan(T.s3[:, 0:512], T.a3[:, 0:512], 512, ta[0])
    tc = more(3, 3, 256, NODES, *tc, *t_hs)
    ta[1] = scan(T.s3[:, 512:1024], T.a3[:, 512:1024], 512, ta[1])
    ta[0] = move("S", in_h(3, 0, 128), T.s3[:, 3:512:4], ta[0], *t_hs)
    pb = own(4, 256, NODES, tc)
    ta[1] = move("V", in_h(3, 128, 256), T.s3[:, 515:1024:4], ta[1])
    pa = [own(5 + k, 128 * k, 128 * k + 128, ta[k]) for k in range(2)]
    t_tab = [move("V", T.u[:, 256:NODES], T.ps[:, 2048:2304], pb), move("S", T.u[:, 0:128], T.ps[:, 2560:2688], pa[0]),
             move("V", T.u[:, 128:256], T.ps[:, 3072:3200], pa[1])]

    a = min(d for d in others if d + 1 in others)
    b = [d for d in others if d not in (a, a + 1)][0]
    ca, cb = C2 * slot(a, r), C2 * (b > a)
    landed = ("a2", 2 * (len(far_eng) + len(near_eng)))
    pb = product(3, T.w2q[:, :], T.w2p[:, :], T.c2[:, cb:cb + 2 * C2], T.p2[:, cb:cb + 2 * C2], 2 * C2, landed)
    pa = product(2, T.w2q[:, :], T.w2p[:, :], T.c2[:, ca:ca + 2 * C2], T.p2[:, ca:ca + 2 * C2], 2 * C2)
    t_tab.append(move("V", T.u[:, NODES + C2 * a:NODES + C2 * (a + 2)], T.ps[:, 1024:1024 + 2 * C2], pa))
    t_tab.append(move("S", T.u[:, NODES + C2 * b:NODES + C2 * (b + 1)], T.ps[:, 1536 + cb:1536 + cb + C2], pb))

    def target(e, k): return T.u[:, 0:W2T].indirect(T.of[:, BY * e + 8 * k:BY * e + 8 * k + 8])
    yb = [T.yb[:, 128 * k:128 * k + 128] for k in range(2)]
    tok = [move(q, yb[k], target(0, k), t_u, *t_tab) for k, q in enumerate("VS")]
    for e in (1, 2, 3):
        for k in range(2):
            need("V", tok[k])
            tok[k] = v(V.tensor_tensor(out=yb[k], in0=target(e, k), in1=yb[k], op=MAX))
    for k, q in enumerate("YS"):
        need(q, tok[k])
        t_y = dma("d_y", queues[q].dma_start(out=T.y[:, 128 * k:128 * k + 128], in_=yb[k]))

    need("g", ("sent", count["sent"]))
    need("Y", *[(k, count[k]) for k in ("cg", "ct", "cs", "cv")], t_y)
